import numpy as np
import ml_dtypes


def mxq(x, axis, fmt="e4m3"):
    dtype, down = {"e4m3": (ml_dtypes.float8_e4m3fn, 7), "e5m2": (ml_dtypes.float8_e5m2, 14)}[fmt]
    v = np.moveaxis(np.asarray(x, np.float32).astype(ml_dtypes.bfloat16).astype(np.float64), axis, -1)
    blocks = v.reshape(v.shape[:-1] + (-1, 32))
    amax = np.abs(blocks).max(-1, keepdims=True)
    byte = np.maximum(np.where(amax > 0, np.frexp(amax)[1] - 1 + 127, 0) - down, 1)
    scale = np.exp2(byte - 127.0)
    codes = (blocks / scale).astype(np.float32).astype(dtype).astype(np.float64)
    return np.moveaxis((codes * scale).reshape(v.shape), -1, axis)


WIDE = False


def mx_kscale(k):
    if not WIDE:
        return np.ones(k)
    levels = np.array([10, -10, 5, -5, 0])
    if k % 512:
        return np.exp2(np.random.permutation(np.resize(levels, k // 32))).repeat(32)
    a = np.empty((k // 512, 16))
    for p in range(k // 512):
        a[p, :8] = np.random.permutation(np.resize(levels, 8))
        for g in range(8):
            far = levels[np.abs(levels - a[p, g]) >= 10]
            a[p, g + 8] = far[np.random.randint(len(far))]
    return np.exp2(a.ravel()).repeat(32)


def f64(x):
    return np.asarray(x).astype(np.float64)


def striped(idx):
    return np.tile(idx.reshape(-1, 16).T, (8, 1)).astype(np.uint16)


def unstriped(offs):
    return offs[:16].T.reshape(-1).astype(np.int64)


def striped8(idx):
    return np.concatenate([x.reshape(-1, 16).T for x in idx]).astype(np.uint16)


def runs(offs, k):
    lists = np.stack([offs[16 * r : 16 * r + 16].T.reshape(-1) for r in range(8)]).astype(np.int64)
    return lists[np.arange(k) % 512 // 64]


def pack_weight(w):
    k, n = w.shape
    w = f64(np.asarray(w, np.float32).astype(ml_dtypes.bfloat16)).reshape(k // 32, 32, n)
    amax = np.abs(w).max(1)
    byte = np.clip(np.where(amax > 0, np.frexp(amax)[1] - 1 + 127 - 7, 1), 1, 254)
    scaled = (w * np.exp2(127.0 - byte)[:, None, :]).reshape(k, n).astype(np.float32)
    words = np.ascontiguousarray(scaled.reshape(k // 512, 128, 4, n).transpose(0, 1, 3, 2)).astype(ml_dtypes.float8_e4m3fn).view(np.uint8)
    return words, np.ascontiguousarray(byte.astype(np.uint8).reshape(k // 512, 16, n))


def unpack_weight(words, scales):
    g, p, n, _ = words.shape
    vals = np.ascontiguousarray(words).view(ml_dtypes.float8_e4m3fn).astype(np.float64) * np.repeat(np.exp2(scales.astype(np.float64) - 127.0), 8, axis=1)[..., None]
    return vals.transpose(0, 1, 3, 2).reshape(g * 512, n)


K, T, S, N, H, J = 512, 2048, 512, 512, 512, 512


def setup_inputs():
    n = np.random.standard_normal
    s = mx_kscale(K)[:, None]
    u = mx_kscale(S)
    packed_xT = pack_weight(n((K, T)) * s)
    return {
        "x_words": packed_xT[0],
        "x_scales": packed_xT[1],
        "wa": (n((K, H)) / np.sqrt(K) / s).astype(np.float32),
        "wb": (n((K, N)) / np.sqrt(K) / s).astype(np.float32),
        "tab": n((S, J)).astype(np.float32),
        "gt": (np.random.uniform(0.5, 1.5, (S, 1)) * u[:, None]).astype(np.float32),
        "gi": (np.random.uniform(0.5, 1.5, (S, 1)) / u[:, None]).astype(np.float32),
        "offs": striped(np.random.permutation(T)[:S]),
        "two": striped(np.random.permutation(T)[:S]),
        "n1": striped8(np.random.randint(0, J, (8, H))),
        "n2": striped8(np.random.randint(0, J, (8, H))),
        "n3": striped8(np.stack([np.random.permutation(H) for _ in range(8)])),
        "n4": striped8(np.stack([np.random.permutation(N) for _ in range(8)])),
        "n5": striped8(np.stack([np.random.permutation(N) for _ in range(8)])),
        "n6": striped8(np.stack([np.random.permutation(N) for _ in range(8)])),
        "n7": striped8(np.stack([np.random.permutation(N) for _ in range(8)])),
        "n8": striped8(np.stack([np.random.permutation(N) for _ in range(8)])),
    }


def reference(x_words, x_scales, wa, wb, tab, gt, gi, offs, two, n1, n2, n3, n4, n5, n6, n7, n8):
    xq = unpack_weight(x_words, x_scales)[:, unstriped(offs)]
    a = xq.T @ mxq(f64(wa), 0, "e4m3")
    z = f64(gt) * ((a[np.arange(S)[:, None], runs(n3, S)]) * (f64(tab)[np.arange(S)[:, None], runs(n1, S)]) + f64(tab)[np.arange(S)[:, None], runs(n2, S)])
    x_two = unpack_weight(x_words, x_scales)[:, unstriped(two)]
    b = x_two.T @ mxq(f64(wb), 0, "e4m3")
    pa = b[np.arange(S)[:, None], runs(n4, S)]
    kr = np.exp(-0.5 * ((b - pa) ** 2))
    pb = b[np.arange(S)[:, None], runs(n5, S)]
    kr2 = np.exp(-0.5 * ((b - pb) ** 2))
    z2 = f64(gi) * ((kr * pa + kr2 * pb) / (kr + kr2 + 0.5))
    cv = 0.0625 * ((mxq(z, 0, "e4m3").T @ mxq(z2, 0, "e4m3")))
    ex = np.exp(0.5 * cv)
    return np.log((ex + ex[np.arange(H)[:, None], runs(n6, H)]) / (ex[np.arange(H)[:, None], runs(n7, H)] + ex[np.arange(H)[:, None], runs(n8, H)]))

@@ -1,0 +1,251 @@
+from contextlib import ExitStack
+
+import concourse.mybir as mybir
+from concourse.masks import make_identity
+
+K, T, S, N, H, J = 512, 2048, 512, 512, 512, 512
+FLOPS = 3 * 2 * 512 * 512 * 512
+
+F32 = mybir.dt.float32
+BF16 = mybir.dt.bfloat16
+I32 = mybir.dt.int32
+U32 = mybir.dt.uint32
+U16 = mybir.dt.uint16
+U8 = mybir.dt.uint8
+FP8X4 = mybir.dt.float8_e4m3fn_x4
+ACT = mybir.ActivationFunctionType
+ALU = mybir.AluOpType
+
+P = 128
+PACK = 4
+W = 512
+WIN = 2 * W
+SCALAR_TILES = 3
+
+
+def tile_picked_mombkindakernodds_none_p_kernel(
+    tc, x_words, x_scales, wa, wb, tab, gt, gi, offs, two, n1, n2, n3, n4, n5, n6, n7, n8, out
+):
+    nc = tc.nc
+    with ExitStack() as ctx:
+        held = ctx.enter_context(tc.tile_pool(name="held", bufs=1))
+        work = ctx.enter_context(tc.tile_pool(name="work", bufs=1))
+        psum = ctx.enter_context(tc.psum_pool(name="psum", bufs=1))
+
+        def load_list(src, name):
+            tile = held.tile([P, W // 16], U16, name=name)
+            nc.sync.dma_start(tile[:], src)
+            return tile
+
+        def window(tag, t):
+            return work.tile([P, WIN], F32, name="%s%d" % (tag, t), tag=tag, bufs=PACK)
+
+        banks = [psum.tile([P, W], F32, name="bank%d" % b) for b in range(8)]
+
+
+        xs = held.tile([P, T], U8, name="xs")
+        nc.vector.memset(xs[:].bitcast(I32), 0)
+        ident = held.tile([P, P], F32, name="ident")
+        make_identity(nc, ident[:])
+
+        tab_rows = tab.rearrange("(p t) j -> p t j", t=PACK)
+        out_rows = out.rearrange("(p t) n -> p t n", t=PACK)
+
+        def load_weight(w, name):
+            raw = work.tile([P, 2, PACK, W // 2], F32, name=name, tag="big", bufs=2)
+            rows = w.rearrange("(p j) (h c) -> p h j c", j=PACK, h=2)
+            for h in range(2):
+                nc.sync.dma_start(raw[:, h], rows[:, h])
+            return raw
+
+        l_two = load_list(two, "l_two")
+        for q in range(4):
+            nc.sync.dma_start(xs[32 * q : 32 * q + 4, :].bitcast(I32), x_scales[0, 4 * q : 4 * q + 4, :].bitcast(I32))
+        l_offs = load_list(offs, "l_offs")
+        wb_raw = load_weight(wb, "wb_raw")
+        xw = held.tile([P, T], U32, name="xw")
+        nc.sync.dma_start(xw[:].bitcast(I32), x_words[0].rearrange("p n r -> p (n r)").bitcast(I32))
+        l4 = load_list(n4, "l4")
+        l5 = load_list(n5, "l5")
+        wa_raw = load_weight(wa, "wa_raw")
+        gts = held.tile([P, PACK], F32, name="gts")
+        nc.sync.dma_start(gts[:], gt.rearrange("(p t) o -> p (t o)", t=PACK))
+        tabw = [window("tabw", t) for t in range(PACK)]
+        for t in range(PACK):
+            nc.sync.dma_start(tabw[t][:, :W], tab_rows[:, t, :])
+        l1 = load_list(n1, "l1")
+        l3 = load_list(n3, "l3")
+        l2 = load_list(n2, "l2")
+        gis = held.tile([P, PACK], F32, name="gis")
+        nc.sync.dma_start(gis[:], gi.rearrange("(p t) o -> p (t o)", t=PACK))
+        l6 = load_list(n6, "l6")
+        l7 = load_list(n7, "l7")
+        l8 = load_list(n8, "l8")
+
+        def quantise(grouped, name):
+            codes = work.tile([P, W], U32, name=name + "_c", align_bytes=64)
+            scales = work.tile([P, W], U8, name=name + "_s", align_bytes=64)
+            nc.vector.quantize_mx(out=codes[:].bitcast(FP8X4), scales=scales[:], in_=grouped)
+            return codes, scales
+
+        def grouped_tile(name):
+            return work.tile([P, W * PACK], BF16, name=name, tag="grouped", bufs=2, align_bytes=64)
+
+        def group_weight(raw, name):
+            grouped = grouped_tile(name)
+            for h in range(2):
+                half = grouped[:, h * 2 * W : (h + 1) * 2 * W]
+                nc.scalar.copy(
+                    half.rearrange("p (c i j) -> p c j i", i=4, j=PACK),
+                    raw[:, h].rearrange("p j (c i) -> p c j i", i=4),
+                )
+            return grouped
+
+        def pick(src, lst, got, name):
+            dtype = got.dtype
+            nc.vector.tensor_copy(got[:], src[:].indirect(lst[:]))
+            dealt = work.tile([P, W], dtype, name=name + "_d", align_bytes=64)
+            nc.vector.tensor_copy(
+                dealt[:].rearrange("p (t m) -> p m t", t=PACK), got[:].rearrange("p (m t) -> p m t", t=PACK)
+            )
+            return dealt
+
+        def product(acc, lhs, rhs, t):
+            cols = slice(t * P, (t + 1) * P)
+            nc.tensor.matmul_mx(
+                out=acc[:],
+                lhsT=lhs[0][:, cols].bitcast(FP8X4),
+                lhsT_scale=lhs[1][:, cols],
+                rhs=rhs[0][:].bitcast(FP8X4),
+                rhs_scale=rhs[1][:],
+                start=True,
+                stop=True,
+            )
+
+        def turn(acc, terms):
+            for c in range(PACK):
+                cols = slice(c * P, (c + 1) * P)
+                for i, term in enumerate(terms):
+                    nc.tensor.matmul(
+                        acc[:, cols], term[:, cols], ident[:], start=(i == 0), stop=(i == len(terms) - 1), is_transpose=True
+                    )
+
+        got_s = work.tile([P, W], U8, name="got_s")
+        got_w = work.tile([P, W], U32, name="got_w")
+        two_s = pick(xs, l_two, got_s, "two_s")
+        offs_s = pick(xs, l_offs, got_s, "offs_s")
+        wb_g = group_weight(wb_raw, "wb_g")
+        wb_q = quantise(wb_g[:], "wb_q")
+        two_w = pick(xw, l_two, got_w, "two_w")
+        bw = [window("bw", t) for t in range(PACK)]
+        nb = work.tile([P, PACK, W], F32, name="nb")
+        for t in range(PACK):
+            product(banks[t], (two_w, two_s), wb_q, t)
+            nc.scalar.activation(bw[t][:, :W], banks[t][:], ACT.Copy)
+        for t in range(PACK):
+            nc.scalar.activation(nb[:, t, :], banks[t][:], ACT.Copy, scale=-1.0)
+        offs_w = pick(xw, l_offs, got_w, "offs_w")
+
+        sq = [work.tile([P, 2, 2, W], F32, name="sq%d" % u, align_bytes=64) for u in range(2)]
+        kr = [work.tile([P, 2, 2, W], F32, name="kr%d" % u) for u in range(2)]
+        pab = [work.tile([P, 2, W], F32, name="pab%d" % t) for t in range(PACK)]
+        for t in range(PACK):
+            for i, lst in enumerate((l4, l5)):
+                nc.vector.tensor_copy(pab[t][:, i, :], bw[t][:].indirect(lst[:]))
+                diff = banks[PACK + (2 * t + i) % PACK]
+                turn(diff, (nb[:, t, :], pab[t][:, i, :]))
+                nc.scalar.activation(sq[t // 2][:, t % 2, i, :], diff[:], ACT.Square)
+            if t % 2 == 1:
+                nc.scalar.activation(
+                    kr[t // 2][:].rearrange("p a b w -> p (a b w)"),
+                    sq[t // 2][:].rearrange("p a b w -> p (a b w)"),
+                    ACT.Exp,
+                    scale=-0.5,
+                )
+
+        wa_g = group_weight(wa_raw, "wa_g")
+        wa_q = quantise(wa_g[:], "wa_q")
+        aw = [window("aw", t) for t in range(PACK)]
+        tabg = [window("tabg", t) for t in range(PACK)]
+        for t in range(PACK):
+            product(banks[PACK + t], (offs_w, offs_s), wa_q, t)
+            nc.scalar.activation(aw[t][:, :W], banks[PACK + t][:], ACT.Copy, scale=gts[:, t : t + 1])
+        for t in range(PACK):
+            nc.scalar.activation(tabg[t][:, :W], tabw[t][:, :W], ACT.Copy, scale=gts[:, t : t + 1])
+
+        weighted = [work.tile([P, 2, 2, W], F32, name="wt%d" % u, tag="big", bufs=2) for u in range(2)]
+
+        def weigh(t, first_bank):
+            for i in range(2):
+                turned = banks[first_bank + 2 * (t % 2) + i]
+                turn(turned, (pab[t][:, i, :],))
+                nc.vector.tensor_tensor(weighted[t // 2][:, t % 2, i, :], turned[:], kr[t // 2][:, t % 2, i, :], ALU.mult)
+
+        for t in range(2):
+            weigh(t, 0)
+        for t in range(PACK):
+            turn(banks[t], (kr[t // 2][:, t % 2, 0, :], kr[t // 2][:, t % 2, 1, :]))
+        lden = sq[1][:].rearrange("p a b w -> p (a b) w")
+        for t in range(PACK):
+            nc.scalar.activation(lden[:, t, :], banks[t][:], ACT.Ln, bias=0.5)
+        rden = sq[0][:].rearrange("p a b w -> p (a b) w")
+        nc.scalar.activation(
+            rden.rearrange("p t w -> p (t w)"), lden.rearrange("p t w -> p (t w)"), ACT.Exp, scale=-1.0
+        )
+
+        z = work.tile([P, PACK, W], F32, name="z")
+        prod = work.tile([P, PACK, W], F32, name="prod")
+        for t in range(PACK):
+            nc.vector.tensor_copy(nb[:, t, :], tabw[t][:].indirect(l1[:]))
+        for t in range(PACK):
+            nc.vector.tensor_tensor(prod[:, t, :], aw[t][:].indirect(l3[:]), nb[:, t, :], ALU.mult)
+            nc.vector.tensor_tensor(z[:, t, :], tabg[t][:].indirect(l2[:]), prod[:, t, :], ALU.add)
+        z_g = lden.rearrange("p t w -> p (t w)").bitcast(BF16)[:, : PACK * W]
+        nc.scalar.copy(
+            z_g.rearrange("p (a m t) -> p m t a", a=PACK, t=PACK),
+            z[:].rearrange("p t (m a) -> p m t a", a=PACK),
+        )
+
+        for t in range(2, PACK):
+            weigh(t, PACK)
+        for t in range(PACK):
+            turn(banks[t], (weighted[t // 2][:, t % 2, 0, :], weighted[t // 2][:, t % 2, 1, :]))
+
+        z2 = work.tile([P, PACK, W], BF16, name="z2")
+        for t in range(PACK):
+            nc.vector.scalar_tensor_tensor(
+                z2[:, t, :], banks[t][:], gis[:, t : t + 1], rden[:, t, :], ALU.mult, ALU.mult
+            )
+        z_q = quantise(z_g, "z_q")
+        z2_g = grouped_tile("z2_g")
+        nc.vector.tensor_copy(
+            z2_g[:].rearrange("p (c i t) -> p c t i", i=4, t=PACK),
+            z2[:].rearrange("p t (c i) -> p c t i", i=4),
+        )
+        z2_q = quantise(z2_g[:], "z2_q")
+
+        exw = [window("tabw", PACK + t) for t in range(PACK)]
+        e6 = nb
+        for t in range(PACK):
+            acc = banks[PACK + t]
+            product(acc, z_q, z2_q, t)
+            nc.scalar.activation(exw[t][:, :W], acc[:], ACT.Exp, scale=0.5 * 0.0625)
+            if t < SCALAR_TILES:
+                nc.scalar.activation(aw[t][:, :W], acc[:], ACT.Copy, scale=0.5 * 0.0625)
+                nc.scalar.activation(e6[:, t, :], aw[t][:].indirect(l6[:]), ACT.Exp)
+            else:
+                nc.scalar.activation(e6[:, t, :], acc[:], ACT.Exp, scale=0.5 * 0.0625)
+        for t in range(PACK):
+            sums = pab[t]
+            nc.vector.tensor_copy(z[:, t, :], exw[t][:].indirect(l7[:]))
+            nc.vector.tensor_tensor(sums[:, 1, :], exw[t][:].indirect(l8[:]), z[:, t, :], ALU.add)
+            if t < SCALAR_TILES:
+                nc.vector.tensor_tensor(sums[:, 0, :], exw[t][:, :W], e6[:, t, :], ALU.add)
+            else:
+                nc.vector.tensor_tensor(sums[:, 0, :], exw[t][:].indirect(l6[:]), e6[:, t, :], ALU.add)
+        for t in range(PACK):
+            logs = kr[t // 2][:, t % 2]
+            for i in range(2):
+                nc.scalar.activation(logs[:, 1 - i, :], pab[t][:, 1 - i, :], ACT.Ln)
+            nc.vector.tensor_tensor(prod[:, t, :], logs[:, 0, :], logs[:, 1, :], ALU.subtract)
+            nc.sync.dma_start(out_rows[:, t, :], prod[:, t, :])

@@ -44,7 +44,7 @@ def tile_picked_mombkindakernodds_none_p_kernel(
 
 
         xs = held.tile([P, T], U8, name="xs")
-        nc.vector.memset(xs[:].bitcast(I32), 0)
+        nc.gpsimd.memset(xs[:].bitcast(I32), 0)
         ident = held.tile([P, P], F32, name="ident")
         make_identity(nc, ident[:])
 
@@ -58,6 +58,7 @@ def tile_picked_mombkindakernodds_none_p_kernel(
                 nc.sync.dma_start(raw[:, h], rows[:, h])
             return raw
 
+        tabw = [window("tabw", t) for t in range(PACK)]
         l_two = load_list(two, "l_two")
         for q in range(4):
             nc.sync.dma_start(xs[32 * q : 32 * q + 4, :].bitcast(I32), x_scales[0, 4 * q : 4 * q + 4, :].bitcast(I32))
@@ -65,15 +66,16 @@ def tile_picked_mombkindakernodds_none_p_kernel(
         wb_raw = load_weight(wb, "wb_raw")
         xw = held.tile([P, T], U32, name="xw")
         nc.sync.dma_start(xw[:].bitcast(I32), x_words[0].rearrange("p n r -> p (n r)").bitcast(I32))
-        l4 = load_list(n4, "l4")
-        l5 = load_list(n5, "l5")
-        wa_raw = load_weight(wa, "wa_raw")
         gts = held.tile([P, PACK], F32, name="gts")
         nc.sync.dma_start(gts[:], gt.rearrange("(p t) o -> p (t o)", t=PACK))
-        tabw = [window("tabw", t) for t in range(PACK)]
-        for t in range(PACK):
-            nc.sync.dma_start(tabw[t][:, :W], tab_rows[:, t, :])
+        wa_raw = load_weight(wa, "wa_raw")
+        l4 = load_list(n4, "l4")
+        l5 = load_list(n5, "l5")
         l1 = load_list(n1, "l1")
+        nc.sync.dma_start(tabw[0][:, :W], tab_rows[:, 0, :])
+        nc.sync.dma_start(tabw[1][:, :W], tab_rows[:, 1, :])
+        for t in range(2, PACK):
+            nc.sync.dma_start(tabw[t][:, :W], tab_rows[:, t, :])
         l3 = load_list(n3, "l3")
         l2 = load_list(n2, "l2")
         gis = held.tile([P, PACK], F32, name="gis")
@@ -82,10 +84,17 @@ def tile_picked_mombkindakernodds_none_p_kernel(
         l7 = load_list(n7, "l7")
         l8 = load_list(n8, "l8")
 
-        def quantise(grouped, name):
+        def quantise(grouped, name, pieces=1):
             codes = work.tile([P, W], U32, name=name + "_c", align_bytes=64)
             scales = work.tile([P, W], U8, name=name + "_s", align_bytes=64)
-            nc.vector.quantize_mx(out=codes[:].bitcast(FP8X4), scales=scales[:], in_=grouped)
+            width = W // pieces
+            for h in range(pieces):
+                cols = slice(h * width, (h + 1) * width)
+                nc.vector.quantize_mx(
+                    out=codes[:, cols].bitcast(FP8X4),
+                    scales=scales[:, cols],
+                    in_=grouped[:, PACK * h * width : PACK * (h + 1) * width],
+                )
             return codes, scales
 
         def grouped_tile(name):
@@ -101,8 +110,9 @@ def tile_picked_mombkindakernodds_none_p_kernel(
                 )
             return grouped
 
-        def pick(src, lst, got, name):
-            dtype = got.dtype
+        def pick(src, lst, dtype, name, got=None):
+            if got is None:
+                got = work.tile([P, W], dtype, name=name + "_g")
             nc.vector.tensor_copy(got[:], src[:].indirect(lst[:]))
             dealt = work.tile([P, W], dtype, name=name + "_d", align_bytes=64)
             nc.vector.tensor_copy(
@@ -110,14 +120,14 @@ def tile_picked_mombkindakernodds_none_p_kernel(
             )
             return dealt
 
-        def product(acc, lhs, rhs, t):
+        def product(acc, lhs, rhs, t, part=slice(0, W)):
             cols = slice(t * P, (t + 1) * P)
             nc.tensor.matmul_mx(
-                out=acc[:],
+                out=acc[:, part],
                 lhsT=lhs[0][:, cols].bitcast(FP8X4),
                 lhsT_scale=lhs[1][:, cols],
-                rhs=rhs[0][:].bitcast(FP8X4),
-                rhs_scale=rhs[1][:],
+                rhs=rhs[0][:, part].bitcast(FP8X4),
+                rhs_scale=rhs[1][:, part],
                 start=True,
                 stop=True,
             )
@@ -130,13 +140,12 @@ def tile_picked_mombkindakernodds_none_p_kernel(
                         acc[:, cols], term[:, cols], ident[:], start=(i == 0), stop=(i == len(terms) - 1), is_transpose=True
                     )
 
-        got_s = work.tile([P, W], U8, name="got_s")
-        got_w = work.tile([P, W], U32, name="got_w")
-        two_s = pick(xs, l_two, got_s, "two_s")
-        offs_s = pick(xs, l_offs, got_s, "offs_s")
+        two_s = pick(xs, l_two, U8, "two_s")
+        offs_s = pick(xs, l_offs, U8, "offs_s")
         wb_g = group_weight(wb_raw, "wb_g")
         wb_q = quantise(wb_g[:], "wb_q")
-        two_w = pick(xw, l_two, got_w, "two_w")
+        got_w = work.tile([P, W], U32, name="got_w")
+        two_w = pick(xw, l_two, U32, "two_w", got_w)
         bw = [window("bw", t) for t in range(PACK)]
         nb = work.tile([P, PACK, W], F32, name="nb")
         for t in range(PACK):
@@ -144,7 +153,7 @@ def tile_picked_mombkindakernodds_none_p_kernel(
             nc.scalar.activation(bw[t][:, :W], banks[t][:], ACT.Copy)
         for t in range(PACK):
             nc.scalar.activation(nb[:, t, :], banks[t][:], ACT.Copy, scale=-1.0)
-        offs_w = pick(xw, l_offs, got_w, "offs_w")
+        offs_w = pick(xw, l_offs, U32, "offs_w", got_w)
 
         sq = [work.tile([P, 2, 2, W], F32, name="sq%d" % u, align_bytes=64) for u in range(2)]
         kr = [work.tile([P, 2, 2, W], F32, name="kr%d" % u) for u in range(2)]
@@ -165,7 +174,7 @@ def tile_picked_mombkindakernodds_none_p_kernel(
 
         wa_g = group_weight(wa_raw, "wa_g")
         wa_q = quantise(wa_g[:], "wa_q")
-        aw = [window("aw", t) for t in range(PACK)]
+        aw = [work.tile([P, WIN + (W if t == 0 else 0)], F32, name="aw%d" % t) for t in range(PACK)]
         tabg = [window("tabg", t) for t in range(PACK)]
         for t in range(PACK):
             product(banks[PACK + t], (offs_w, offs_s), wa_q, t)
@@ -198,7 +207,8 @@ def tile_picked_mombkindakernodds_none_p_kernel(
         for t in range(PACK):
             nc.vector.tensor_copy(nb[:, t, :], tabw[t][:].indirect(l1[:]))
         for t in range(PACK):
-            nc.vector.tensor_tensor(prod[:, t, :], aw[t][:].indirect(l3[:]), nb[:, t, :], ALU.mult)
+            picked = nb[:, t, :]
+            nc.vector.tensor_tensor(prod[:, t, :], aw[t][:].indirect(l3[:]), picked, ALU.mult)
             nc.vector.tensor_tensor(z[:, t, :], tabg[t][:].indirect(l2[:]), prod[:, t, :], ALU.add)
         z_g = lden.rearrange("p t w -> p (t w)").bitcast(BF16)[:, : PACK * W]
         nc.scalar.copy(
@@ -216,36 +226,43 @@ def tile_picked_mombkindakernodds_none_p_kernel(
             nc.vector.scalar_tensor_tensor(
                 z2[:, t, :], banks[t][:], gis[:, t : t + 1], rden[:, t, :], ALU.mult, ALU.mult
             )
-        z_q = quantise(z_g, "z_q")
         z2_g = grouped_tile("z2_g")
-        nc.vector.tensor_copy(
-            z2_g[:].rearrange("p (c i t) -> p c t i", i=4, t=PACK),
-            z2[:].rearrange("p t (c i) -> p c t i", i=4),
-        )
-        z2_q = quantise(z2_g[:], "z2_q")
+        for h, copy in enumerate((nc.vector.tensor_copy, nc.scalar.copy)):
+            copy(
+                z2_g[:, h * 2 * W : (h + 1) * 2 * W].rearrange("p (c i t) -> p c t i", i=4, t=PACK),
+                z2[:, :, h * (W // 2) : (h + 1) * (W // 2)].rearrange("p t (c i) -> p c t i", i=4),
+            )
+        z2_q = quantise(z2_g[:], "z2_q", 2)
+        z_q = quantise(z_g, "z_q", 2)
 
         exw = [window("tabw", PACK + t) for t in range(PACK)]
         e6 = nb
+        pieces = [[(banks[PACK + t], slice(0, W))] for t in range(PACK)]
+        pieces[0] = [(banks[PACK], slice(0, W // 2)), (banks[0], slice(W // 2, W))]
         for t in range(PACK):
-            acc = banks[PACK + t]
-            product(acc, z_q, z2_q, t)
-            nc.scalar.activation(exw[t][:, :W], acc[:], ACT.Exp, scale=0.5 * 0.0625)
+            for acc, part in pieces[t]:
+                product(acc, z_q, z2_q, t, part)
+                nc.scalar.activation(exw[t][:, part], acc[:, part], ACT.Exp, scale=0.5 * 0.0625)
+        for t in range(PACK):
+            for acc, part in pieces[t]:
+                if t < SCALAR_TILES:
+                    nc.scalar.activation(aw[t][:, part], acc[:, part], ACT.Copy, scale=0.5 * 0.0625)
+                else:
+                    nc.scalar.activation(e6[:, t, part], acc[:, part], ACT.Exp, scale=0.5 * 0.0625)
             if t < SCALAR_TILES:
-                nc.scalar.activation(aw[t][:, :W], acc[:], ACT.Copy, scale=0.5 * 0.0625)
                 nc.scalar.activation(e6[:, t, :], aw[t][:].indirect(l6[:]), ACT.Exp)
-            else:
-                nc.scalar.activation(e6[:, t, :], acc[:], ACT.Exp, scale=0.5 * 0.0625)
+        lower = [aw[t][:, W:WIN] for t in range(SCALAR_TILES)] + [aw[0][:, WIN:]]
         for t in range(PACK):
-            sums = pab[t]
             nc.vector.tensor_copy(z[:, t, :], exw[t][:].indirect(l7[:]))
-            nc.vector.tensor_tensor(sums[:, 1, :], exw[t][:].indirect(l8[:]), z[:, t, :], ALU.add)
+        for t in range(PACK):
+            nc.vector.tensor_tensor(lower[t], exw[t][:].indirect(l8[:]), z[:, t, :], ALU.add)
             if t < SCALAR_TILES:
-                nc.vector.tensor_tensor(sums[:, 0, :], exw[t][:, :W], e6[:, t, :], ALU.add)
+                nc.vector.tensor_tensor(pab[t][:, 0, :], exw[t][:, :W], e6[:, t, :], ALU.add)
             else:
-                nc.vector.tensor_tensor(sums[:, 0, :], exw[t][:].indirect(l6[:]), e6[:, t, :], ALU.add)
+                nc.vector.tensor_tensor(pab[t][:, 0, :], exw[t][:].indirect(l6[:]), e6[:, t, :], ALU.add)
         for t in range(PACK):
             logs = kr[t // 2][:, t % 2]
-            for i in range(2):
-                nc.scalar.activation(logs[:, 1 - i, :], pab[t][:, 1 - i, :], ACT.Ln)
+            nc.scalar.activation(logs[:, 1, :], lower[t], ACT.Ln)
+            nc.scalar.activation(logs[:, 0, :], pab[t][:, 0, :], ACT.Ln)
             nc.vector.tensor_tensor(prod[:, t, :], logs[:, 0, :], logs[:, 1, :], ALU.subtract)
             nc.sync.dma_start(out_rows[:, t, :], prod[:, t, :])

@@ -20,7 +20,7 @@ P = 128
 PACK = 4
 W = 512
 WIN = 2 * W
-SCALAR_TILES = 3
+VECTOR_TILES = 1
 
 
 def tile_picked_mombkindakernodds_none_p_kernel(
@@ -51,30 +51,30 @@ def tile_picked_mombkindakernodds_none_p_kernel(
         tab_rows = tab.rearrange("(p t) j -> p t j", t=PACK)
         out_rows = out.rearrange("(p t) n -> p t n", t=PACK)
 
-        def load_weight(w, name):
-            raw = work.tile([P, 2, PACK, W // 2], F32, name=name, tag="big", bufs=2)
+        def load_half(raw, w, h):
             rows = w.rearrange("(p j) (h c) -> p h j c", j=PACK, h=2)
-            for h in range(2):
-                nc.sync.dma_start(raw[:, h], rows[:, h])
-            return raw
+            nc.sync.dma_start(raw[:, h], rows[:, h])
 
         tabw = [window("tabw", t) for t in range(PACK)]
         l_two = load_list(two, "l_two")
         for q in range(4):
             nc.sync.dma_start(xs[32 * q : 32 * q + 4, :].bitcast(I32), x_scales[0, 4 * q : 4 * q + 4, :].bitcast(I32))
         l_offs = load_list(offs, "l_offs")
-        wb_raw = load_weight(wb, "wb_raw")
         xw = held.tile([P, T], U32, name="xw")
         nc.sync.dma_start(xw[:].bitcast(I32), x_words[0].rearrange("p n r -> p (n r)").bitcast(I32))
-        gts = held.tile([P, PACK], F32, name="gts")
-        nc.sync.dma_start(gts[:], gt.rearrange("(p t) o -> p (t o)", t=PACK))
-        wa_raw = load_weight(wa, "wa_raw")
-        l4 = load_list(n4, "l4")
-        l5 = load_list(n5, "l5")
+        wb_raw = work.tile([P, 2, PACK, W // 2], F32, name="wb_raw", tag="big", bufs=2)
+        wa_raw = work.tile([P, 2, PACK, W // 2], F32, name="wa_raw", tag="big", bufs=2)
+        load_half(wb_raw, wb, 0)
+        load_half(wb_raw, wb, 1)
         l1 = load_list(n1, "l1")
         nc.sync.dma_start(tabw[0][:, :W], tab_rows[:, 0, :])
-        nc.sync.dma_start(tabw[1][:, :W], tab_rows[:, 1, :])
-        for t in range(2, PACK):
+        load_half(wa_raw, wa, 0)
+        load_half(wa_raw, wa, 1)
+        l4 = load_list(n4, "l4")
+        l5 = load_list(n5, "l5")
+        gts = held.tile([P, PACK], F32, name="gts")
+        nc.sync.dma_start(gts[:], gt.rearrange("(p t) o -> p (t o)", t=PACK))
+        for t in range(1, PACK):
             nc.sync.dma_start(tabw[t][:, :W], tab_rows[:, t, :])
         l3 = load_list(n3, "l3")
         l2 = load_list(n2, "l2")
@@ -110,9 +110,8 @@ def tile_picked_mombkindakernodds_none_p_kernel(
                 )
             return grouped
 
-        def pick(src, lst, dtype, name, got=None):
-            if got is None:
-                got = work.tile([P, W], dtype, name=name + "_g")
+        def pick(src, lst, dtype, name):
+            got = work.tile([P, W], dtype, name=name + "_g")
             nc.vector.tensor_copy(got[:], src[:].indirect(lst[:]))
             dealt = work.tile([P, W], dtype, name=name + "_d", align_bytes=64)
             nc.vector.tensor_copy(
@@ -143,17 +142,21 @@ def tile_picked_mombkindakernodds_none_p_kernel(
         two_s = pick(xs, l_two, U8, "two_s")
         offs_s = pick(xs, l_offs, U8, "offs_s")
         wb_g = group_weight(wb_raw, "wb_g")
-        wb_q = quantise(wb_g[:], "wb_q")
-        got_w = work.tile([P, W], U32, name="got_w")
-        two_w = pick(xw, l_two, U32, "two_w", got_w)
+        wa_g = group_weight(wa_raw, "wa_g")
+        wb_q = quantise(wb_g[:], "wb_q", 2)
+        two_w = pick(xw, l_two, U32, "two_w")
         bw = [window("bw", t) for t in range(PACK)]
         nb = work.tile([P, PACK, W], F32, name="nb")
         for t in range(PACK):
             product(banks[t], (two_w, two_s), wb_q, t)
             nc.scalar.activation(bw[t][:, :W], banks[t][:], ACT.Copy)
-        for t in range(PACK):
+            if t == 0:
+                nc.scalar.activation(nb[:, t, :], banks[t][:], ACT.Copy, scale=-1.0)
+        for t in range(1, PACK):
             nc.scalar.activation(nb[:, t, :], banks[t][:], ACT.Copy, scale=-1.0)
-        offs_w = pick(xw, l_offs, U32, "offs_w", got_w)
+        offs_w = pick(xw, l_offs, U32, "offs_w")
+        tab_first = wb_g[:, 2 * W :].bitcast(F32)
+        nc.vector.tensor_copy(tab_first, tabw[0][:].indirect(l1[:]))
 
         sq = [work.tile([P, 2, 2, W], F32, name="sq%d" % u, align_bytes=64) for u in range(2)]
         kr = [work.tile([P, 2, 2, W], F32, name="kr%d" % u) for u in range(2)]
@@ -172,9 +175,8 @@ def tile_picked_mombkindakernodds_none_p_kernel(
                     scale=-0.5,
                 )
 
-        wa_g = group_weight(wa_raw, "wa_g")
         wa_q = quantise(wa_g[:], "wa_q")
-        aw = [work.tile([P, WIN + (W if t == 0 else 0)], F32, name="aw%d" % t) for t in range(PACK)]
+        aw = [work.tile([P, WIN + (WIN if t == VECTOR_TILES else 0)], F32, name="aw%d" % t) for t in range(PACK)]
         tabg = [window("tabg", t) for t in range(PACK)]
         for t in range(PACK):
             product(banks[PACK + t], (offs_w, offs_s), wa_q, t)
@@ -204,10 +206,10 @@ def tile_picked_mombkindakernodds_none_p_kernel(
 
         z = work.tile([P, PACK, W], F32, name="z")
         prod = work.tile([P, PACK, W], F32, name="prod")
-        for t in range(PACK):
+        for t in range(1, PACK):
             nc.vector.tensor_copy(nb[:, t, :], tabw[t][:].indirect(l1[:]))
         for t in range(PACK):
-            picked = nb[:, t, :]
+            picked = nb[:, t, :] if t else tab_first
             nc.vector.tensor_tensor(prod[:, t, :], aw[t][:].indirect(l3[:]), picked, ALU.mult)
             nc.vector.tensor_tensor(z[:, t, :], tabg[t][:].indirect(l2[:]), prod[:, t, :], ALU.add)
         z_g = lden.rearrange("p t w -> p (t w)").bitcast(BF16)[:, : PACK * W]
@@ -243,26 +245,29 @@ def tile_picked_mombkindakernodds_none_p_kernel(
             for acc, part in pieces[t]:
                 product(acc, z_q, z2_q, t, part)
                 nc.scalar.activation(exw[t][:, part], acc[:, part], ACT.Exp, scale=0.5 * 0.0625)
-        for t in range(PACK):
-            for acc, part in pieces[t]:
-                if t < SCALAR_TILES:
-                    nc.scalar.activation(aw[t][:, part], acc[:, part], ACT.Copy, scale=0.5 * 0.0625)
-                else:
-                    nc.scalar.activation(e6[:, t, part], acc[:, part], ACT.Exp, scale=0.5 * 0.0625)
-            if t < SCALAR_TILES:
-                nc.scalar.activation(e6[:, t, :], aw[t][:].indirect(l6[:]), ACT.Exp)
-        lower = [aw[t][:, W:WIN] for t in range(SCALAR_TILES)] + [aw[0][:, WIN:]]
+        for t in range(VECTOR_TILES, PACK - 1):
+            nc.scalar.activation(aw[t][:, :W], banks[PACK + t][:], ACT.Copy, scale=0.5 * 0.0625)
+        nc.vector.tensor_scalar(aw[PACK - 1][:, :W], banks[2 * PACK - 1][:], 0.5 * 0.0625, None, ALU.mult)
+        for t in range(VECTOR_TILES, PACK):
+            nc.scalar.activation(e6[:, t, :], aw[t][:].indirect(l6[:]), ACT.Exp)
+        first = aw[VECTOR_TILES]
+        lower = [first[:, W:WIN], first[:, WIN : WIN + W], first[:, WIN + W :], aw[PACK - 1][:, W:WIN]]
         for t in range(PACK):
             nc.vector.tensor_copy(z[:, t, :], exw[t][:].indirect(l7[:]))
+            if t < VECTOR_TILES:
+                nc.vector.tensor_copy(e6[:, t, :], exw[t][:].indirect(l6[:]))
         for t in range(PACK):
             nc.vector.tensor_tensor(lower[t], exw[t][:].indirect(l8[:]), z[:, t, :], ALU.add)
-            if t < SCALAR_TILES:
-                nc.vector.tensor_tensor(pab[t][:, 0, :], exw[t][:, :W], e6[:, t, :], ALU.add)
-            else:
-                nc.vector.tensor_tensor(pab[t][:, 0, :], exw[t][:].indirect(l6[:]), e6[:, t, :], ALU.add)
+        whole = (slice(0, W),)
+        halves = (slice(0, W // 2), slice(W // 2, W))
+        upper = [banks[(t + 1) % PACK] for t in range(PACK)]
+        for t in range(PACK):
+            turn(upper[t], (e6[:, t, :], exw[t][:, :W]))
         for t in range(PACK):
             logs = kr[t // 2][:, t % 2]
-            nc.scalar.activation(logs[:, 1, :], lower[t], ACT.Ln)
-            nc.scalar.activation(logs[:, 0, :], pab[t][:, 0, :], ACT.Ln)
-            nc.vector.tensor_tensor(prod[:, t, :], logs[:, 0, :], logs[:, 1, :], ALU.subtract)
-            nc.sync.dma_start(out_rows[:, t, :], prod[:, t, :])
+            nc.scalar.activation(logs[:, 0, :], upper[t][:], ACT.Ln)
+            turn(banks[PACK + t], (logs[:, 0, :],))
+            for part in halves if t == PACK - 1 else whole:
+                nc.scalar.activation(logs[:, 1, part], lower[t][:, part], ACT.Ln)
+                nc.vector.tensor_tensor(prod[:, t, part], banks[PACK + t][:, part], logs[:, 1, part], ALU.subtract)
+                nc.sync.dma_start(out_rows[:, t, part], prod[:, t, part])

@@ -3,9 +3,6 @@ from contextlib import ExitStack
 import concourse.mybir as mybir
 from concourse.masks import make_identity
 
-K, T, S, N, H, J = 512, 2048, 512, 512, 512, 512
-FLOPS = 3 * 2 * 512 * 512 * 512
-
 F32 = mybir.dt.float32
 BF16 = mybir.dt.bfloat16
 I32 = mybir.dt.int32
@@ -19,8 +16,13 @@ ALU = mybir.AluOpType
 P = 128
 PACK = 4
 W = 512
-WIN = 2 * W
+HALF = W // 2
+TOKENS = 2048
+WINDOW = 2 * W
+CV_SCALE = 0.5 * 0.0625
 VECTOR_TILES = 1
+
+FLOPS = 3 * 2 * W * W * W
 
 
 def tile_picked_mombkindakernodds_none_p_kernel(
@@ -32,242 +34,262 @@ def tile_picked_mombkindakernodds_none_p_kernel(
         work = ctx.enter_context(tc.tile_pool(name="work", bufs=1))
         psum = ctx.enter_context(tc.psum_pool(name="psum", bufs=1))
 
+        banks = [psum.tile([P, W], F32, name="bank%d" % b) for b in range(2 * PACK)]
+        low, high = banks[:PACK], banks[PACK:]
+        halves = (slice(0, HALF), slice(HALF, W))
+        whole = (slice(0, W),)
+
         def load_list(src, name):
             tile = held.tile([P, W // 16], U16, name=name)
             nc.sync.dma_start(tile[:], src)
             return tile
 
-        def window(tag, t):
-            return work.tile([P, WIN], F32, name="%s%d" % (tag, t), tag=tag, bufs=PACK)
+        def load_column(src, name):
+            tile = held.tile([P, PACK], F32, name=name)
+            nc.sync.dma_start(tile[:], src.rearrange("(p t) o -> p (t o)", t=PACK))
+            return tile
 
-        banks = [psum.tile([P, W], F32, name="bank%d" % b) for b in range(8)]
+        def load_half(raw, weight, h):
+            nc.sync.dma_start(raw[:, h], weight.rearrange("(p j) (h c) -> p h j c", j=PACK, h=2)[:, h])
 
+        def windows(tag, first=0):
+            return [work.tile([P, WINDOW], F32, name="%s%d" % (tag, first + t), tag=tag, bufs=PACK) for t in range(PACK)]
 
-        xs = held.tile([P, T], U8, name="xs")
-        nc.gpsimd.memset(xs[:].bitcast(I32), 0)
-        ident = held.tile([P, P], F32, name="ident")
-        make_identity(nc, ident[:])
-
-        tab_rows = tab.rearrange("(p t) j -> p t j", t=PACK)
-        out_rows = out.rearrange("(p t) n -> p t n", t=PACK)
-
-        def load_half(raw, w, h):
-            rows = w.rearrange("(p j) (h c) -> p h j c", j=PACK, h=2)
-            nc.sync.dma_start(raw[:, h], rows[:, h])
-
-        tabw = [window("tabw", t) for t in range(PACK)]
-        l_two = load_list(two, "l_two")
-        for q in range(4):
-            nc.sync.dma_start(xs[32 * q : 32 * q + 4, :].bitcast(I32), x_scales[0, 4 * q : 4 * q + 4, :].bitcast(I32))
-        l_offs = load_list(offs, "l_offs")
-        xw = held.tile([P, T], U32, name="xw")
-        nc.sync.dma_start(xw[:].bitcast(I32), x_words[0].rearrange("p n r -> p (n r)").bitcast(I32))
-        wb_raw = work.tile([P, 2, PACK, W // 2], F32, name="wb_raw", tag="big", bufs=2)
-        wa_raw = work.tile([P, 2, PACK, W // 2], F32, name="wa_raw", tag="big", bufs=2)
-        load_half(wb_raw, wb, 0)
-        load_half(wb_raw, wb, 1)
-        l1 = load_list(n1, "l1")
-        nc.sync.dma_start(tabw[0][:, :W], tab_rows[:, 0, :])
-        load_half(wa_raw, wa, 0)
-        load_half(wa_raw, wa, 1)
-        l4 = load_list(n4, "l4")
-        l5 = load_list(n5, "l5")
-        gts = held.tile([P, PACK], F32, name="gts")
-        nc.sync.dma_start(gts[:], gt.rearrange("(p t) o -> p (t o)", t=PACK))
-        for t in range(1, PACK):
-            nc.sync.dma_start(tabw[t][:, :W], tab_rows[:, t, :])
-        l3 = load_list(n3, "l3")
-        l2 = load_list(n2, "l2")
-        gis = held.tile([P, PACK], F32, name="gis")
-        nc.sync.dma_start(gis[:], gi.rearrange("(p t) o -> p (t o)", t=PACK))
-        l6 = load_list(n6, "l6")
-        l7 = load_list(n7, "l7")
-        l8 = load_list(n8, "l8")
-
-        def quantise(grouped, name, pieces=1):
-            codes = work.tile([P, W], U32, name=name + "_c", align_bytes=64)
-            scales = work.tile([P, W], U8, name=name + "_s", align_bytes=64)
-            width = W // pieces
-            for h in range(pieces):
-                cols = slice(h * width, (h + 1) * width)
-                nc.vector.quantize_mx(
-                    out=codes[:, cols].bitcast(FP8X4),
-                    scales=scales[:, cols],
-                    in_=grouped[:, PACK * h * width : PACK * (h + 1) * width],
-                )
-            return codes, scales
+        def pair_tile(name):
+            return work.tile([P, 2, 2, W], F32, name=name, tag="pair", bufs=2)
 
         def grouped_tile(name):
             return work.tile([P, W * PACK], BF16, name=name, tag="grouped", bufs=2, align_bytes=64)
 
-        def group_weight(raw, name):
-            grouped = grouped_tile(name)
-            for h in range(2):
-                half = grouped[:, h * 2 * W : (h + 1) * 2 * W]
-                nc.scalar.copy(
-                    half.rearrange("p (c i j) -> p c j i", i=4, j=PACK),
-                    raw[:, h].rearrange("p j (c i) -> p c j i", i=4),
-                )
-            return grouped
+        def group(copy, grouped, start, planes):
+            width = planes.shape[2]
+            copy(
+                grouped[:, PACK * start : PACK * (start + width)].rearrange("p (c i j) -> p c j i", i=4, j=PACK),
+                planes.rearrange("p j (c i) -> p c j i", i=4),
+            )
 
-        def pick(src, lst, dtype, name):
-            got = work.tile([P, W], dtype, name=name + "_g")
-            nc.vector.tensor_copy(got[:], src[:].indirect(lst[:]))
-            dealt = work.tile([P, W], dtype, name=name + "_d", align_bytes=64)
+        def quantise(grouped, name, widths):
+            codes = work.tile([P, W], U32, name=name + "_codes", align_bytes=64)
+            scales = work.tile([P, W], U8, name=name + "_scales", align_bytes=64)
+            start = 0
+            for width in widths:
+                cols = slice(start, start + width)
+                nc.vector.quantize_mx(
+                    out=codes[:, cols].bitcast(FP8X4),
+                    scales=scales[:, cols],
+                    in_=grouped[:, PACK * start : PACK * (start + width)],
+                )
+                start = start + width
+            return codes, scales
+
+        def pick(table, entries, dtype, name):
+            picked = work.tile([P, W], dtype, name=name + "_picked")
+            nc.vector.tensor_copy(picked[:], table[:].indirect(entries[:]))
+            dealt = work.tile([P, W], dtype, name=name + "_dealt", align_bytes=64)
             nc.vector.tensor_copy(
-                dealt[:].rearrange("p (t m) -> p m t", t=PACK), got[:].rearrange("p (m t) -> p m t", t=PACK)
+                dealt[:].rearrange("p (t m) -> p m t", t=PACK), picked[:].rearrange("p (m t) -> p m t", t=PACK)
             )
             return dealt
 
-        def product(acc, lhs, rhs, t, part=slice(0, W)):
+        def product(bank, stationary, moving, t, part=whole[0]):
             cols = slice(t * P, (t + 1) * P)
             nc.tensor.matmul_mx(
-                out=acc[:, part],
-                lhsT=lhs[0][:, cols].bitcast(FP8X4),
-                lhsT_scale=lhs[1][:, cols],
-                rhs=rhs[0][:, part].bitcast(FP8X4),
-                rhs_scale=rhs[1][:, part],
+                out=bank[:, part],
+                lhsT=stationary[0][:, cols].bitcast(FP8X4),
+                lhsT_scale=stationary[1][:, cols],
+                rhs=moving[0][:, part].bitcast(FP8X4),
+                rhs_scale=moving[1][:, part],
                 start=True,
                 stop=True,
             )
 
-        def turn(acc, terms):
+        def turn(bank, *terms):
             for c in range(PACK):
                 cols = slice(c * P, (c + 1) * P)
                 for i, term in enumerate(terms):
                     nc.tensor.matmul(
-                        acc[:, cols], term[:, cols], ident[:], start=(i == 0), stop=(i == len(terms) - 1), is_transpose=True
+                        bank[:, cols],
+                        term[:, cols],
+                        identity[:],
+                        start=(i == 0),
+                        stop=(i == len(terms) - 1),
+                        is_transpose=True,
                     )
 
-        two_s = pick(xs, l_two, U8, "two_s")
-        offs_s = pick(xs, l_offs, U8, "offs_s")
-        wb_g = group_weight(wb_raw, "wb_g")
-        wa_g = group_weight(wa_raw, "wa_g")
-        wb_q = quantise(wb_g[:], "wb_q", 2)
-        two_w = pick(xw, l_two, U32, "two_w")
-        bw = [window("bw", t) for t in range(PACK)]
-        nb = work.tile([P, PACK, W], F32, name="nb")
-        for t in range(PACK):
-            product(banks[t], (two_w, two_s), wb_q, t)
-            nc.scalar.activation(bw[t][:, :W], banks[t][:], ACT.Copy)
-            if t == 0:
-                nc.scalar.activation(nb[:, t, :], banks[t][:], ACT.Copy, scale=-1.0)
-        for t in range(1, PACK):
-            nc.scalar.activation(nb[:, t, :], banks[t][:], ACT.Copy, scale=-1.0)
-        offs_w = pick(xw, l_offs, U32, "offs_w")
-        tab_first = wb_g[:, 2 * W :].bitcast(F32)
-        nc.vector.tensor_copy(tab_first, tabw[0][:].indirect(l1[:]))
+        scale_table = held.tile([P, TOKENS], U8, name="scale_table")
+        nc.gpsimd.memset(scale_table[:].bitcast(I32), 0)
+        identity = held.tile([P, P], F32, name="identity")
+        make_identity(nc, identity[:])
 
-        sq = [work.tile([P, 2, 2, W], F32, name="sq%d" % u, align_bytes=64) for u in range(2)]
-        kr = [work.tile([P, 2, 2, W], F32, name="kr%d" % u) for u in range(2)]
-        pab = [work.tile([P, 2, W], F32, name="pab%d" % t) for t in range(PACK)]
+        tab_rows = tab.rearrange("(p t) j -> p t j", t=PACK)
+        out_rows = out.rearrange("(p t) n -> p t n", t=PACK)
+        tab_windows = windows("tab_or_ex")
+        list_two = load_list(two, "list_two")
+        for q in range(P // 32):
+            nc.sync.dma_start(
+                scale_table[32 * q : 32 * q + 4, :].bitcast(I32), x_scales[0, 4 * q : 4 * q + 4, :].bitcast(I32)
+            )
+        list_offs = load_list(offs, "list_offs")
+        word_table = held.tile([P, TOKENS], U32, name="word_table")
+        nc.sync.dma_start(word_table[:].bitcast(I32), x_words[0].rearrange("p n r -> p (n r)").bitcast(I32))
+        wb_raw = pair_tile("wb_raw")[:].rearrange("p h a (b c) -> p h (a b) c", b=2)
+        wa_raw = pair_tile("wa_raw")[:].rearrange("p h a (b c) -> p h (a b) c", b=2)
+        load_half(wb_raw, wb, 0)
+        load_half(wb_raw, wb, 1)
+        list1 = load_list(n1, "list1")
+        nc.sync.dma_start(tab_windows[0][:, :W], tab_rows[:, 0, :])
+        load_half(wa_raw, wa, 0)
+        load_half(wa_raw, wa, 1)
+        list4 = load_list(n4, "list4")
+        list5 = load_list(n5, "list5")
+        gt_column = load_column(gt, "gt_column")
+        for t in range(1, PACK):
+            nc.sync.dma_start(tab_windows[t][:, :W], tab_rows[:, t, :])
+        list3 = load_list(n3, "list3")
+        list2 = load_list(n2, "list2")
+        gi_column = load_column(gi, "gi_column")
+        list6 = load_list(n6, "list6")
+        list7 = load_list(n7, "list7")
+        list8 = load_list(n8, "list8")
+
+        two_scales = pick(scale_table, list_two, U8, "two_scales")
+        offs_scales = pick(scale_table, list_offs, U8, "offs_scales")
+        wb_grouped = grouped_tile("wb_grouped")
+        wa_grouped = grouped_tile("wa_grouped")
+        group(nc.scalar.copy, wb_grouped, 0, wb_raw[:, 0])
+        group(nc.scalar.copy, wb_grouped, HALF, wb_raw[:, 1])
+        group(nc.scalar.copy, wa_grouped, 0, wa_raw[:, 0])
+        wb_mx = quantise(wb_grouped, "wb", (HALF, HALF))
+        two_words = pick(word_table, list_two, U32, "two_words")
+        b_windows = windows("b")
+        minus_b = work.tile([P, PACK, W], F32, name="minus_b")
         for t in range(PACK):
-            for i, lst in enumerate((l4, l5)):
-                nc.vector.tensor_copy(pab[t][:, i, :], bw[t][:].indirect(lst[:]))
-                diff = banks[PACK + (2 * t + i) % PACK]
-                turn(diff, (nb[:, t, :], pab[t][:, i, :]))
-                nc.scalar.activation(sq[t // 2][:, t % 2, i, :], diff[:], ACT.Square)
+            product(low[t], (two_words, two_scales), wb_mx, t)
+            nc.scalar.activation(b_windows[t][:, :W], low[t][:], ACT.Copy)
+            if t == 1:
+                nc.scalar.activation(minus_b[:, 0, :], low[0][:], ACT.Copy, scale=-1.0)
+                group(nc.scalar.copy, wa_grouped, HALF, wa_raw[:, 1])
+        for t in range(1, PACK):
+            nc.scalar.activation(minus_b[:, t, :], low[t][:], ACT.Copy, scale=-1.0)
+        offs_words = pick(word_table, list_offs, U32, "offs_words")
+        tab1_first = wb_grouped[:, 2 * W :].bitcast(F32)
+        nc.vector.tensor_copy(tab1_first, tab_windows[0][:].indirect(list1[:]))
+
+        squares = [work.tile([P, 2, 2, W], F32, name="squares%d" % u, align_bytes=64) for u in range(2)]
+        kernels = [work.tile([P, 2, 2, W], F32, name="kernels%d" % u) for u in range(2)]
+        partners = [work.tile([P, 2, W], F32, name="partners%d" % t) for t in range(PACK)]
+        for t in range(PACK):
+            for i, entries in enumerate((list4, list5)):
+                nc.vector.tensor_copy(partners[t][:, i, :], b_windows[t][:].indirect(entries[:]))
+                difference = high[2 * (t % 2) + i]
+                turn(difference, minus_b[:, t, :], partners[t][:, i, :])
+                nc.scalar.activation(squares[t // 2][:, t % 2, i, :], difference[:], ACT.Square)
             if t % 2 == 1:
                 nc.scalar.activation(
-                    kr[t // 2][:].rearrange("p a b w -> p (a b w)"),
-                    sq[t // 2][:].rearrange("p a b w -> p (a b w)"),
+                    kernels[t // 2][:].rearrange("p a b w -> p (a b w)"),
+                    squares[t // 2][:].rearrange("p a b w -> p (a b w)"),
                     ACT.Exp,
                     scale=-0.5,
                 )
 
-        wa_q = quantise(wa_g[:], "wa_q")
-        aw = [work.tile([P, WIN + (WIN if t == VECTOR_TILES else 0)], F32, name="aw%d" % t) for t in range(PACK)]
-        tabg = [window("tabg", t) for t in range(PACK)]
+        wa_mx = quantise(wa_grouped, "wa", (W,))
+        a_windows = [
+            work.tile([P, 2 * WINDOW if t == VECTOR_TILES else WINDOW], F32, name="a%d" % t) for t in range(PACK)
+        ]
+        gt_tab_windows = windows("gt_tab")
         for t in range(PACK):
-            product(banks[PACK + t], (offs_w, offs_s), wa_q, t)
-            nc.scalar.activation(aw[t][:, :W], banks[PACK + t][:], ACT.Copy, scale=gts[:, t : t + 1])
+            product(high[t], (offs_words, offs_scales), wa_mx, t)
+            nc.scalar.activation(a_windows[t][:, :W], high[t][:], ACT.Copy, scale=gt_column[:, t : t + 1])
         for t in range(PACK):
-            nc.scalar.activation(tabg[t][:, :W], tabw[t][:, :W], ACT.Copy, scale=gts[:, t : t + 1])
+            nc.scalar.activation(
+                gt_tab_windows[t][:, :W], tab_windows[t][:, :W], ACT.Copy, scale=gt_column[:, t : t + 1]
+            )
 
-        weighted = [work.tile([P, 2, 2, W], F32, name="wt%d" % u, tag="big", bufs=2) for u in range(2)]
+        weighted = [pair_tile("weighted%d" % u) for u in range(2)]
 
-        def weigh(t, first_bank):
+        def weigh(t, four_banks):
             for i in range(2):
-                turned = banks[first_bank + 2 * (t % 2) + i]
-                turn(turned, (pab[t][:, i, :],))
-                nc.vector.tensor_tensor(weighted[t // 2][:, t % 2, i, :], turned[:], kr[t // 2][:, t % 2, i, :], ALU.mult)
+                turned = four_banks[2 * (t % 2) + i]
+                turn(turned, partners[t][:, i, :])
+                nc.vector.tensor_tensor(
+                    weighted[t // 2][:, t % 2, i, :], turned[:], kernels[t // 2][:, t % 2, i, :], ALU.mult
+                )
 
         for t in range(2):
-            weigh(t, 0)
+            weigh(t, low)
         for t in range(PACK):
-            turn(banks[t], (kr[t // 2][:, t % 2, 0, :], kr[t // 2][:, t % 2, 1, :]))
-        lden = sq[1][:].rearrange("p a b w -> p (a b) w")
+            turn(low[t], kernels[t // 2][:, t % 2, 0, :], kernels[t // 2][:, t % 2, 1, :])
+        log_denominator = squares[1][:].rearrange("p a b w -> p (a b) w")
         for t in range(PACK):
-            nc.scalar.activation(lden[:, t, :], banks[t][:], ACT.Ln, bias=0.5)
-        rden = sq[0][:].rearrange("p a b w -> p (a b) w")
+            nc.scalar.activation(log_denominator[:, t, :], low[t][:], ACT.Ln, bias=0.5)
+        reciprocal = squares[0][:].rearrange("p a b w -> p (a b) w")
         nc.scalar.activation(
-            rden.rearrange("p t w -> p (t w)"), lden.rearrange("p t w -> p (t w)"), ACT.Exp, scale=-1.0
+            reciprocal.rearrange("p t w -> p (t w)"), log_denominator.rearrange("p t w -> p (t w)"), ACT.Exp, scale=-1.0
         )
 
         z = work.tile([P, PACK, W], F32, name="z")
-        prod = work.tile([P, PACK, W], F32, name="prod")
+        a_tab = work.tile([P, PACK, W], F32, name="a_tab")
+        tab1 = [tab1_first] + [minus_b[:, t, :] for t in range(1, PACK)]
         for t in range(1, PACK):
-            nc.vector.tensor_copy(nb[:, t, :], tabw[t][:].indirect(l1[:]))
+            nc.vector.tensor_copy(tab1[t], tab_windows[t][:].indirect(list1[:]))
         for t in range(PACK):
-            picked = nb[:, t, :] if t else tab_first
-            nc.vector.tensor_tensor(prod[:, t, :], aw[t][:].indirect(l3[:]), picked, ALU.mult)
-            nc.vector.tensor_tensor(z[:, t, :], tabg[t][:].indirect(l2[:]), prod[:, t, :], ALU.add)
-        z_g = lden.rearrange("p t w -> p (t w)").bitcast(BF16)[:, : PACK * W]
+            nc.vector.tensor_tensor(a_tab[:, t, :], a_windows[t][:].indirect(list3[:]), tab1[t], ALU.mult)
+        for t in range(PACK):
+            nc.vector.tensor_tensor(z[:, t, :], gt_tab_windows[t][:].indirect(list2[:]), a_tab[:, t, :], ALU.add)
+        z_grouped = log_denominator.rearrange("p t w -> p (t w)").bitcast(BF16)[:, : PACK * W]
         nc.scalar.copy(
-            z_g.rearrange("p (a m t) -> p m t a", a=PACK, t=PACK),
+            z_grouped.rearrange("p (a m t) -> p m t a", a=PACK, t=PACK),
             z[:].rearrange("p t (m a) -> p m t a", a=PACK),
         )
 
         for t in range(2, PACK):
-            weigh(t, PACK)
+            weigh(t, high)
         for t in range(PACK):
-            turn(banks[t], (weighted[t // 2][:, t % 2, 0, :], weighted[t // 2][:, t % 2, 1, :]))
-
+            turn(low[t], weighted[t // 2][:, t % 2, 0, :], weighted[t // 2][:, t % 2, 1, :])
         z2 = work.tile([P, PACK, W], BF16, name="z2")
         for t in range(PACK):
             nc.vector.scalar_tensor_tensor(
-                z2[:, t, :], banks[t][:], gis[:, t : t + 1], rden[:, t, :], ALU.mult, ALU.mult
+                z2[:, t, :], low[t][:], gi_column[:, t : t + 1], reciprocal[:, t, :], ALU.mult, ALU.mult
             )
-        z2_g = grouped_tile("z2_g")
-        for h, copy in enumerate((nc.vector.tensor_copy, nc.scalar.copy)):
-            copy(
-                z2_g[:, h * 2 * W : (h + 1) * 2 * W].rearrange("p (c i t) -> p c t i", i=4, t=PACK),
-                z2[:, :, h * (W // 2) : (h + 1) * (W // 2)].rearrange("p t (c i) -> p c t i", i=4),
-            )
-        z2_q = quantise(z2_g[:], "z2_q", 2)
-        z_q = quantise(z_g, "z_q", 2)
+        z2_grouped = grouped_tile("z2_grouped")
+        for part, copy in zip(halves, (nc.vector.tensor_copy, nc.scalar.copy)):
+            group(copy, z2_grouped, part.start, z2[:, :, part])
+        z2_mx = quantise(z2_grouped, "z2", (HALF, HALF))
+        z_mx = quantise(z_grouped, "z", (P, P, 2 * P))
 
-        exw = [window("tabw", PACK + t) for t in range(PACK)]
-        e6 = nb
-        pieces = [[(banks[PACK + t], slice(0, W))] for t in range(PACK)]
-        pieces[0] = [(banks[PACK], slice(0, W // 2)), (banks[0], slice(W // 2, W))]
+        ex_windows = windows("tab_or_ex", PACK)
+        cv_windows = a_windows
+        ex6 = minus_b
+        ex7 = z
+        pieces = [list(zip((high[0], low[0]), halves))] + [[(high[t], whole[0])] for t in range(1, PACK)]
         for t in range(PACK):
-            for acc, part in pieces[t]:
-                product(acc, z_q, z2_q, t, part)
-                nc.scalar.activation(exw[t][:, part], acc[:, part], ACT.Exp, scale=0.5 * 0.0625)
+            for bank, part in pieces[t]:
+                product(bank, z_mx, z2_mx, t, part)
+                nc.scalar.activation(ex_windows[t][:, part], bank[:, part], ACT.Exp, scale=CV_SCALE)
         for t in range(VECTOR_TILES, PACK - 1):
-            nc.scalar.activation(aw[t][:, :W], banks[PACK + t][:], ACT.Copy, scale=0.5 * 0.0625)
-        nc.vector.tensor_scalar(aw[PACK - 1][:, :W], banks[2 * PACK - 1][:], 0.5 * 0.0625, None, ALU.mult)
+            nc.scalar.activation(cv_windows[t][:, :W], high[t][:], ACT.Copy, scale=CV_SCALE)
+        nc.vector.tensor_scalar(cv_windows[PACK - 1][:, :W], high[PACK - 1][:], CV_SCALE, None, ALU.mult)
         for t in range(VECTOR_TILES, PACK):
-            nc.scalar.activation(e6[:, t, :], aw[t][:].indirect(l6[:]), ACT.Exp)
-        first = aw[VECTOR_TILES]
-        lower = [first[:, W:WIN], first[:, WIN : WIN + W], first[:, WIN + W :], aw[PACK - 1][:, W:WIN]]
+            nc.scalar.activation(ex6[:, t, :], cv_windows[t][:].indirect(list6[:]), ACT.Exp)
+
+        wide = cv_windows[VECTOR_TILES]
+        lower = [wide[:, (t + 1) * W : (t + 2) * W] for t in range(PACK - 1)] + [cv_windows[PACK - 1][:, W:]]
         for t in range(PACK):
-            nc.vector.tensor_copy(z[:, t, :], exw[t][:].indirect(l7[:]))
+            nc.vector.tensor_copy(ex7[:, t, :], ex_windows[t][:].indirect(list7[:]))
             if t < VECTOR_TILES:
-                nc.vector.tensor_copy(e6[:, t, :], exw[t][:].indirect(l6[:]))
+                nc.vector.tensor_copy(ex6[:, t, :], ex_windows[t][:].indirect(list6[:]))
         for t in range(PACK):
-            nc.vector.tensor_tensor(lower[t], exw[t][:].indirect(l8[:]), z[:, t, :], ALU.add)
-        whole = (slice(0, W),)
-        halves = (slice(0, W // 2), slice(W // 2, W))
-        upper = [banks[(t + 1) % PACK] for t in range(PACK)]
+            nc.vector.tensor_tensor(lower[t], ex_windows[t][:].indirect(list8[:]), ex7[:, t, :], ALU.add)
+        upper = low[1:] + low[:1]
+        logs = [kernels[t // 2][:, t % 2] for t in range(PACK)]
+        result = a_tab
         for t in range(PACK):
-            turn(upper[t], (e6[:, t, :], exw[t][:, :W]))
+            turn(upper[t], ex6[:, t, :], ex_windows[t][:, :W])
         for t in range(PACK):
-            logs = kr[t // 2][:, t % 2]
-            nc.scalar.activation(logs[:, 0, :], upper[t][:], ACT.Ln)
-            turn(banks[PACK + t], (logs[:, 0, :],))
+            nc.scalar.activation(logs[t][:, 0, :], upper[t][:], ACT.Ln)
+            turn(high[t], logs[t][:, 0, :])
+        for t in range(PACK):
             for part in halves if t == PACK - 1 else whole:
-                nc.scalar.activation(logs[:, 1, part], lower[t][:, part], ACT.Ln)
-                nc.vector.tensor_tensor(prod[:, t, part], banks[PACK + t][:, part], logs[:, 1, part], ALU.subtract)
-                nc.sync.dma_start(out_rows[:, t, part], prod[:, t, part])
+                nc.scalar.activation(logs[t][:, 1, part], lower[t][:, part], ACT.Ln)
+                nc.vector.tensor_tensor(result[:, t, part], high[t][:, part], logs[t][:, 1, part], ALU.subtract)
+                nc.sync.dma_start(out_rows[:, t, part], result[:, t, part])

@@ -20,7 +20,7 @@ HALF = W // 2
 TOKENS = 2048
 WINDOW = 2 * W
 CV_SCALE = 0.5 * 0.0625
-VECTOR_TILES = 1
+SCALAR_FROM = 2
 
 FLOPS = 3 * 2 * W * W * W
 
@@ -55,8 +55,8 @@ def tile_picked_mombkindakernodds_none_p_kernel(
         def windows(tag, first=0):
             return [work.tile([P, WINDOW], F32, name="%s%d" % (tag, first + t), tag=tag, bufs=PACK) for t in range(PACK)]
 
-        def pair_tile(name):
-            return work.tile([P, 2, 2, W], F32, name=name, tag="pair", bufs=2)
+        def large_tile(name, shape):
+            return work.tile(shape, F32, name=name, tag="large", bufs=2)
 
         def grouped_tile(name):
             return work.tile([P, W * PACK], BF16, name=name, tag="grouped", bufs=2, align_bytes=64)
@@ -68,19 +68,24 @@ def tile_picked_mombkindakernodds_none_p_kernel(
                 planes.rearrange("p j (c i) -> p c j i", i=4),
             )
 
-        def quantise(grouped, name, widths):
+        def group_weight(raw, name):
+            grouped = grouped_tile(name)
+            for h, part in enumerate(halves):
+                group(nc.scalar.copy, grouped, part.start, raw[:, h])
+            return grouped
+
+        def mx_tiles(name):
             codes = work.tile([P, W], U32, name=name + "_codes", align_bytes=64)
             scales = work.tile([P, W], U8, name=name + "_scales", align_bytes=64)
-            start = 0
-            for width in widths:
-                cols = slice(start, start + width)
-                nc.vector.quantize_mx(
-                    out=codes[:, cols].bitcast(FP8X4),
-                    scales=scales[:, cols],
-                    in_=grouped[:, PACK * start : PACK * (start + width)],
-                )
-                start = start + width
             return codes, scales
+
+        def quantise(operand, grouped, start, width):
+            cols = slice(start, start + width)
+            nc.vector.quantize_mx(
+                out=operand[0][:, cols].bitcast(FP8X4),
+                scales=operand[1][:, cols],
+                in_=grouped[:, PACK * start : PACK * (start + width)],
+            )
 
         def pick(table, entries, dtype, name):
             picked = work.tile([P, W], dtype, name=name + "_picked")
@@ -132,8 +137,8 @@ def tile_picked_mombkindakernodds_none_p_kernel(
         list_offs = load_list(offs, "list_offs")
         word_table = held.tile([P, TOKENS], U32, name="word_table")
         nc.sync.dma_start(word_table[:].bitcast(I32), x_words[0].rearrange("p n r -> p (n r)").bitcast(I32))
-        wb_raw = pair_tile("wb_raw")[:].rearrange("p h a (b c) -> p h (a b) c", b=2)
-        wa_raw = pair_tile("wa_raw")[:].rearrange("p h a (b c) -> p h (a b) c", b=2)
+        wb_raw = large_tile("wb_raw", [P, 2, PACK, HALF])
+        wa_raw = large_tile("wa_raw", [P, 2, PACK, HALF])
         load_half(wb_raw, wb, 0)
         load_half(wb_raw, wb, 1)
         list1 = load_list(n1, "list1")
@@ -154,141 +159,165 @@ def tile_picked_mombkindakernodds_none_p_kernel(
 
         two_scales = pick(scale_table, list_two, U8, "two_scales")
         offs_scales = pick(scale_table, list_offs, U8, "offs_scales")
-        wb_grouped = grouped_tile("wb_grouped")
-        wa_grouped = grouped_tile("wa_grouped")
-        group(nc.scalar.copy, wb_grouped, 0, wb_raw[:, 0])
-        group(nc.scalar.copy, wb_grouped, HALF, wb_raw[:, 1])
-        group(nc.scalar.copy, wa_grouped, 0, wa_raw[:, 0])
-        wb_mx = quantise(wb_grouped, "wb", (HALF, HALF))
+        wb_grouped = group_weight(wb_raw, "wb_grouped")
+        wa_grouped = group_weight(wa_raw, "wa_grouped")
+        wb_mx = mx_tiles("wb")
+        for part in halves:
+            quantise(wb_mx, wb_grouped, part.start, HALF)
         two_words = pick(word_table, list_two, U32, "two_words")
         b_windows = windows("b")
-        minus_b = work.tile([P, PACK, W], F32, name="minus_b")
         for t in range(PACK):
             product(low[t], (two_words, two_scales), wb_mx, t)
             nc.scalar.activation(b_windows[t][:, :W], low[t][:], ACT.Copy)
-            if t == 1:
-                nc.scalar.activation(minus_b[:, 0, :], low[0][:], ACT.Copy, scale=-1.0)
-                group(nc.scalar.copy, wa_grouped, HALF, wa_raw[:, 1])
-        for t in range(1, PACK):
-            nc.scalar.activation(minus_b[:, t, :], low[t][:], ACT.Copy, scale=-1.0)
         offs_words = pick(word_table, list_offs, U32, "offs_words")
         tab1_first = wb_grouped[:, 2 * W :].bitcast(F32)
         nc.vector.tensor_copy(tab1_first, tab_windows[0][:].indirect(list1[:]))
 
-        squares = [work.tile([P, 2, 2, W], F32, name="squares%d" % u, align_bytes=64) for u in range(2)]
-        kernels = [work.tile([P, 2, 2, W], F32, name="kernels%d" % u) for u in range(2)]
+        squares = [work.tile([P, PACK, W], F32, name="squares%d" % u, align_bytes=64) for u in range(2)]
+        z_and_kernels = work.tile([P, PACK + 1, W], F32, name="z_and_kernels")
+        kernels = [work.tile([P, PACK, W], F32, name="kernels")[:], z_and_kernels[:, 1:, :]]
+
+        def slot(t, i):
+            return (2 * (t % 2) + i - 1) % PACK
+
         partners = [work.tile([P, 2, W], F32, name="partners%d" % t) for t in range(PACK)]
+
+        def gauss(u):
+            nc.scalar.activation(
+                kernels[u].rearrange("p s w -> p (s w)"),
+                squares[u][:].rearrange("p s w -> p (s w)"),
+                ACT.Exp,
+                scale=-0.5,
+            )
+
         for t in range(PACK):
             for i, entries in enumerate((list4, list5)):
-                nc.vector.tensor_copy(partners[t][:, i, :], b_windows[t][:].indirect(entries[:]))
-                difference = high[2 * (t % 2) + i]
-                turn(difference, minus_b[:, t, :], partners[t][:, i, :])
-                nc.scalar.activation(squares[t // 2][:, t % 2, i, :], difference[:], ACT.Square)
-            if t % 2 == 1:
-                nc.scalar.activation(
-                    kernels[t // 2][:].rearrange("p a b w -> p (a b w)"),
-                    squares[t // 2][:].rearrange("p a b w -> p (a b w)"),
-                    ACT.Exp,
-                    scale=-0.5,
+                nc.vector.tensor_scalar(
+                    partners[t][:, i, :], b_windows[t][:].indirect(entries[:]), -1.0, 0.0, ALU.mult, ALU.add
                 )
+                difference = high[2 * (t % 2) + i]
+                turn(difference, partners[t][:, i, :], b_windows[t][:, :W])
+                nc.scalar.activation(squares[t // 2][:, slot(t, i), :], difference[:], ACT.Square)
+            if t == 1:
+                gauss(0)
 
-        wa_mx = quantise(wa_grouped, "wa", (W,))
-        a_windows = [
-            work.tile([P, 2 * WINDOW if t == VECTOR_TILES else WINDOW], F32, name="a%d" % t) for t in range(PACK)
-        ]
+        wa_mx = mx_tiles("wa")
+        quantise(wa_mx, wa_grouped, 0, W)
+        a_windows = windows("a")
         gt_tab_windows = windows("gt_tab")
         for t in range(PACK):
-            product(high[t], (offs_words, offs_scales), wa_mx, t)
-            nc.scalar.activation(a_windows[t][:, :W], high[t][:], ACT.Copy, scale=gt_column[:, t : t + 1])
-        for t in range(PACK):
+            product(low[t], (offs_words, offs_scales), wa_mx, t)
+            nc.scalar.activation(a_windows[t][:, :W], low[t][:], ACT.Copy, scale=gt_column[:, t : t + 1])
+        gauss(1)
+        for t in reversed(range(PACK)):
             nc.scalar.activation(
                 gt_tab_windows[t][:, :W], tab_windows[t][:, :W], ACT.Copy, scale=gt_column[:, t : t + 1]
             )
 
-        weighted = [pair_tile("weighted%d" % u) for u in range(2)]
+        weighted = [large_tile("weighted%d" % u, [P, 2, 2, W]) for u in range(2)]
 
-        def weigh(t, four_banks):
+        for t in range(PACK):
+            turn(low[t], kernels[t // 2][:, slot(t, 0), :], kernels[t // 2][:, slot(t, 1), :])
+        for t in range(PACK):
             for i in range(2):
-                turned = four_banks[2 * (t % 2) + i]
+                turned = high[2 * (t % 2) + i]
                 turn(turned, partners[t][:, i, :])
                 nc.vector.tensor_tensor(
-                    weighted[t // 2][:, t % 2, i, :], turned[:], kernels[t // 2][:, t % 2, i, :], ALU.mult
+                    weighted[t // 2][:, t % 2, i, :], turned[:], kernels[t // 2][:, slot(t, i), :], ALU.mult
                 )
-
-        for t in range(2):
-            weigh(t, low)
-        for t in range(PACK):
-            turn(low[t], kernels[t // 2][:, t % 2, 0, :], kernels[t // 2][:, t % 2, 1, :])
-        log_denominator = squares[1][:].rearrange("p a b w -> p (a b) w")
+        log_denominator = squares[1]
         for t in range(PACK):
             nc.scalar.activation(log_denominator[:, t, :], low[t][:], ACT.Ln, bias=0.5)
-        reciprocal = squares[0][:].rearrange("p a b w -> p (a b) w")
+        reciprocal = squares[0]
         nc.scalar.activation(
-            reciprocal.rearrange("p t w -> p (t w)"), log_denominator.rearrange("p t w -> p (t w)"), ACT.Exp, scale=-1.0
+            reciprocal[:].rearrange("p t w -> p (t w)"),
+            log_denominator[:].rearrange("p t w -> p (t w)"),
+            ACT.Exp,
+            scale=-1.0,
         )
+        minus_gi = held.tile([P, PACK], F32, name="minus_gi")
+        nc.scalar.activation(minus_gi[:], gi_column[:], ACT.Copy, scale=-1.0)
+        factor = log_denominator
+        for t in range(PACK):
+            nc.scalar.activation(factor[:, t, :], reciprocal[:, t, :], ACT.Copy, scale=minus_gi[:, t : t + 1])
 
-        z = work.tile([P, PACK, W], F32, name="z")
+        z = z_and_kernels[:, :PACK, :]
         a_tab = work.tile([P, PACK, W], F32, name="a_tab")
-        tab1 = [tab1_first] + [minus_b[:, t, :] for t in range(1, PACK)]
+        tab1 = [tab1_first] + [b_windows[t][:, :W] for t in range(1, PACK)]
         for t in range(1, PACK):
             nc.vector.tensor_copy(tab1[t], tab_windows[t][:].indirect(list1[:]))
         for t in range(PACK):
             nc.vector.tensor_tensor(a_tab[:, t, :], a_windows[t][:].indirect(list3[:]), tab1[t], ALU.mult)
-        for t in range(PACK):
-            nc.vector.tensor_tensor(z[:, t, :], gt_tab_windows[t][:].indirect(list2[:]), a_tab[:, t, :], ALU.add)
-        z_grouped = log_denominator.rearrange("p t w -> p (t w)").bitcast(BF16)[:, : PACK * W]
-        nc.scalar.copy(
-            z_grouped.rearrange("p (a m t) -> p m t a", a=PACK, t=PACK),
-            z[:].rearrange("p t (m a) -> p m t a", a=PACK),
-        )
-
-        for t in range(2, PACK):
-            weigh(t, high)
-        for t in range(PACK):
-            turn(low[t], weighted[t // 2][:, t % 2, 0, :], weighted[t // 2][:, t % 2, 1, :])
-        z2 = work.tile([P, PACK, W], BF16, name="z2")
-        for t in range(PACK):
-            nc.vector.scalar_tensor_tensor(
-                z2[:, t, :], low[t][:], gi_column[:, t : t + 1], reciprocal[:, t, :], ALU.mult, ALU.mult
+            for part in halves if t == PACK - 1 else whole:
+                entries = list2[:, part.start // 16 : part.stop // 16]
+                nc.vector.tensor_tensor(
+                    z[:, t, part], gt_tab_windows[t][:].indirect(entries), a_tab[:, t, part], ALU.add
+                )
+        z_grouped = reciprocal[:].rearrange("p t w -> p (t w)").bitcast(BF16)[:, : PACK * W]
+        for h, part in enumerate(halves):
+            nc.scalar.copy(
+                z_grouped.rearrange("p (a h m t) -> p h m t a", a=PACK, h=2, t=PACK)[:, h],
+                z[:, :, part].rearrange("p t (m a) -> p m t a", a=PACK),
             )
+
+        for t in range(PACK):
+            for c in range(PACK):
+                for i in range(2):
+                    nc.tensor.matmul(
+                        low[c][:, t * P : (t + 1) * P],
+                        weighted[t // 2][:, t % 2, i, c * P : (c + 1) * P],
+                        identity[:],
+                        start=(i == 0),
+                        stop=(i == 1),
+                        is_transpose=True,
+                    )
         z2_grouped = grouped_tile("z2_grouped")
-        for part, copy in zip(halves, (nc.vector.tensor_copy, nc.scalar.copy)):
-            group(copy, z2_grouped, part.start, z2[:, :, part])
-        z2_mx = quantise(z2_grouped, "z2", (HALF, HALF))
-        z_mx = quantise(z_grouped, "z", (P, P, 2 * P))
+        for c in range(PACK):
+            nc.vector.tensor_tensor(
+                z2_grouped[:, c * W : (c + 1) * W].rearrange("p (c i t) -> p c t i", i=4, t=PACK),
+                low[c][:].rearrange("p (t c i) -> p c t i", i=4, t=PACK),
+                factor[:, :, c * P : (c + 1) * P].rearrange("p t (c i) -> p c t i", i=4),
+                ALU.mult,
+            )
+        z_mx = mx_tiles("z")
+        z2_mx = mx_tiles("z2")
+        quantise(z2_mx, z2_grouped, 0, HALF)
+        quantise(z_mx, z_grouped, 0, P)
+        quantise(z2_mx, z2_grouped, HALF, HALF)
+        quantise(z_mx, z_grouped, P, P)
+        quantise(z_mx, z_grouped, HALF, HALF)
 
         ex_windows = windows("tab_or_ex", PACK)
         cv_windows = a_windows
-        ex6 = minus_b
-        ex7 = z
+        ex6 = [b_windows[t][:, :W] for t in range(PACK)]
+        ex7 = factor
         pieces = [list(zip((high[0], low[0]), halves))] + [[(high[t], whole[0])] for t in range(1, PACK)]
         for t in range(PACK):
             for bank, part in pieces[t]:
                 product(bank, z_mx, z2_mx, t, part)
                 nc.scalar.activation(ex_windows[t][:, part], bank[:, part], ACT.Exp, scale=CV_SCALE)
-        for t in range(VECTOR_TILES, PACK - 1):
+        last = PACK - 1
+        for t in range(SCALAR_FROM, PACK):
             nc.scalar.activation(cv_windows[t][:, :W], high[t][:], ACT.Copy, scale=CV_SCALE)
-        nc.vector.tensor_scalar(cv_windows[PACK - 1][:, :W], high[PACK - 1][:], CV_SCALE, None, ALU.mult)
-        for t in range(VECTOR_TILES, PACK):
-            nc.scalar.activation(ex6[:, t, :], cv_windows[t][:].indirect(list6[:]), ACT.Exp)
+        for t in range(SCALAR_FROM, PACK):
+            nc.scalar.activation(ex6[t], cv_windows[t][:].indirect(list6[:]), ACT.Exp)
+        nc.scalar.activation(ex7[:, last, :], cv_windows[last][:].indirect(list7[:]), ACT.Exp)
 
-        wide = cv_windows[VECTOR_TILES]
-        lower = [wide[:, (t + 1) * W : (t + 2) * W] for t in range(PACK - 1)] + [cv_windows[PACK - 1][:, W:]]
-        for t in range(PACK):
+        lower = [partners[t][:, 0, :] for t in range(PACK)]
+        for t in range(last):
             nc.vector.tensor_copy(ex7[:, t, :], ex_windows[t][:].indirect(list7[:]))
-            if t < VECTOR_TILES:
-                nc.vector.tensor_copy(ex6[:, t, :], ex_windows[t][:].indirect(list6[:]))
+            if t < SCALAR_FROM:
+                nc.vector.tensor_copy(ex6[t], ex_windows[t][:].indirect(list6[:]))
         for t in range(PACK):
             nc.vector.tensor_tensor(lower[t], ex_windows[t][:].indirect(list8[:]), ex7[:, t, :], ALU.add)
         upper = low[1:] + low[:1]
-        logs = [kernels[t // 2][:, t % 2] for t in range(PACK)]
+        logs = [kernels[t // 2][:, 2 * (t % 2) : 2 * (t % 2) + 2, :] for t in range(PACK)]
         result = a_tab
         for t in range(PACK):
-            turn(upper[t], ex6[:, t, :], ex_windows[t][:, :W])
+            turn(upper[t], ex6[t], ex_windows[t][:, :W])
         for t in range(PACK):
             nc.scalar.activation(logs[t][:, 0, :], upper[t][:], ACT.Ln)
             turn(high[t], logs[t][:, 0, :])
-        for t in range(PACK):
             for part in halves if t == PACK - 1 else whole:
                 nc.scalar.activation(logs[t][:, 1, part], lower[t][:, part], ACT.Ln)
                 nc.vector.tensor_tensor(result[:, t, part], high[t][:, part], logs[t][:, 1, part], ALU.subtract)

from contextlib import ExitStack

import concourse.mybir as mybir
from concourse.masks import make_identity

F32 = mybir.dt.float32
BF16 = mybir.dt.bfloat16
I32 = mybir.dt.int32
U32 = mybir.dt.uint32
U16 = mybir.dt.uint16
U8 = mybir.dt.uint8
FP8X4 = mybir.dt.float8_e4m3fn_x4
ACT = mybir.ActivationFunctionType
ALU = mybir.AluOpType

P = 128
PACK = 4
W = 512
HALF = W // 2
TOKENS = 2048
WINDOW = 2 * W
CV_SCALE = 0.5 * 0.0625
SCALAR_FROM = 2

FLOPS = 3 * 2 * W * W * W


def tile_picked_mombkindakernodds_none_p_kernel(
    tc, x_words, x_scales, wa, wb, tab, gt, gi, offs, two, n1, n2, n3, n4, n5, n6, n7, n8, out
):
    nc = tc.nc
    with ExitStack() as ctx:
        held = ctx.enter_context(tc.tile_pool(name="held", bufs=1))
        work = ctx.enter_context(tc.tile_pool(name="work", bufs=1))
        psum = ctx.enter_context(tc.psum_pool(name="psum", bufs=1))

        banks = [psum.tile([P, W], F32, name="bank%d" % b) for b in range(2 * PACK)]
        low, high = banks[:PACK], banks[PACK:]
        halves = (slice(0, HALF), slice(HALF, W))
        whole = (slice(0, W),)

        def load_list(src, name):
            tile = held.tile([P, W // 16], U16, name=name)
            nc.sync.dma_start(tile[:], src)
            return tile

        def load_column(src, name):
            tile = held.tile([P, PACK], F32, name=name)
            nc.sync.dma_start(tile[:], src.rearrange("(p t) o -> p (t o)", t=PACK))
            return tile

        def load_half(raw, weight, h):
            nc.sync.dma_start(raw[:, h], weight.rearrange("(p j) (h c) -> p h j c", j=PACK, h=2)[:, h])

        def windows(tag, first=0):
            return [work.tile([P, WINDOW], F32, name="%s%d" % (tag, first + t), tag=tag, bufs=PACK) for t in range(PACK)]

        def large_tile(name, shape):
            return work.tile(shape, F32, name=name, tag="large", bufs=2)

        def grouped_tile(name):
            return work.tile([P, W * PACK], BF16, name=name, tag="grouped", bufs=2, align_bytes=64)

        def group(copy, grouped, start, planes):
            width = planes.shape[2]
            copy(
                grouped[:, PACK * start : PACK * (start + width)].rearrange("p (c i j) -> p c j i", i=4, j=PACK),
                planes.rearrange("p j (c i) -> p c j i", i=4),
            )

        def group_weight(raw, name):
            grouped = grouped_tile(name)
            for h, part in enumerate(halves):
                group(nc.scalar.copy, grouped, part.start, raw[:, h])
            return grouped

        def mx_tiles(name):
            codes = work.tile([P, W], U32, name=name + "_codes", align_bytes=64)
            scales = work.tile([P, W], U8, name=name + "_scales", align_bytes=64)
            return codes, scales

        def quantise(operand, grouped, start, width):
            cols = slice(start, start + width)
            nc.vector.quantize_mx(
                out=operand[0][:, cols].bitcast(FP8X4),
                scales=operand[1][:, cols],
                in_=grouped[:, PACK * start : PACK * (start + width)],
            )

        def pick(table, entries, dtype, name):
            picked = work.tile([P, W], dtype, name=name + "_picked")
            nc.vector.tensor_copy(picked[:], table[:].indirect(entries[:]))
            dealt = work.tile([P, W], dtype, name=name + "_dealt", align_bytes=64)
            nc.vector.tensor_copy(
                dealt[:].rearrange("p (t m) -> p m t", t=PACK), picked[:].rearrange("p (m t) -> p m t", t=PACK)
            )
            return dealt

        def product(bank, stationary, moving, t, part=whole[0]):
            cols = slice(t * P, (t + 1) * P)
            nc.tensor.matmul_mx(
                out=bank[:, part],
                lhsT=stationary[0][:, cols].bitcast(FP8X4),
                lhsT_scale=stationary[1][:, cols],
                rhs=moving[0][:, part].bitcast(FP8X4),
                rhs_scale=moving[1][:, part],
                start=True,
                stop=True,
            )

        def turn(bank, *terms):
            for c in range(PACK):
                cols = slice(c * P, (c + 1) * P)
                for i, term in enumerate(terms):
                    nc.tensor.matmul(
                        bank[:, cols],
                        term[:, cols],
                        identity[:],
                        start=(i == 0),
                        stop=(i == len(terms) - 1),
                        is_transpose=True,
                    )

        scale_table = held.tile([P, TOKENS], U8, name="scale_table")
        nc.gpsimd.memset(scale_table[:].bitcast(I32), 0)
        identity = held.tile([P, P], F32, name="identity")
        make_identity(nc, identity[:])

        tab_rows = tab.rearrange("(p t) j -> p t j", t=PACK)
        out_rows = out.rearrange("(p t) n -> p t n", t=PACK)
        tab_windows = windows("tab_or_ex")
        list_two = load_list(two, "list_two")
        for q in range(P // 32):
            nc.sync.dma_start(
                scale_table[32 * q : 32 * q + 4, :].bitcast(I32), x_scales[0, 4 * q : 4 * q + 4, :].bitcast(I32)
            )
        list_offs = load_list(offs, "list_offs")
        word_table = held.tile([P, TOKENS], U32, name="word_table")
        nc.sync.dma_start(word_table[:].bitcast(I32), x_words[0].rearrange("p n r -> p (n r)").bitcast(I32))
        wb_raw = large_tile("wb_raw", [P, 2, PACK, HALF])
        wa_raw = large_tile("wa_raw", [P, 2, PACK, HALF])
        load_half(wb_raw, wb, 0)
        load_half(wb_raw, wb, 1)
        list1 = load_list(n1, "list1")
        nc.sync.dma_start(tab_windows[0][:, :W], tab_rows[:, 0, :])
        load_half(wa_raw, wa, 0)
        load_half(wa_raw, wa, 1)
        list4 = load_list(n4, "list4")
        list5 = load_list(n5, "list5")
        gt_column = load_column(gt, "gt_column")
        for t in range(1, PACK):
            nc.sync.dma_start(tab_windows[t][:, :W], tab_rows[:, t, :])
        list3 = load_list(n3, "list3")
        list2 = load_list(n2, "list2")
        gi_column = load_column(gi, "gi_column")
        list6 = load_list(n6, "list6")
        list7 = load_list(n7, "list7")
        list8 = load_list(n8, "list8")

        two_scales = pick(scale_table, list_two, U8, "two_scales")
        offs_scales = pick(scale_table, list_offs, U8, "offs_scales")
        wb_grouped = group_weight(wb_raw, "wb_grouped")
        wa_grouped = group_weight(wa_raw, "wa_grouped")
        wb_mx = mx_tiles("wb")
        for part in halves:
            quantise(wb_mx, wb_grouped, part.start, HALF)
        two_words = pick(word_table, list_two, U32, "two_words")
        b_windows = windows("b")
        for t in range(PACK):
            product(low[t], (two_words, two_scales), wb_mx, t)
            nc.scalar.activation(b_windows[t][:, :W], low[t][:], ACT.Copy)
        offs_words = pick(word_table, list_offs, U32, "offs_words")
        tab1_first = wb_grouped[:, 2 * W :].bitcast(F32)
        nc.vector.tensor_copy(tab1_first, tab_windows[0][:].indirect(list1[:]))

        squares = [work.tile([P, PACK, W], F32, name="squares%d" % u, align_bytes=64) for u in range(2)]
        z_and_kernels = work.tile([P, PACK + 1, W], F32, name="z_and_kernels")
        kernels = [work.tile([P, PACK, W], F32, name="kernels")[:], z_and_kernels[:, 1:, :]]

        def slot(t, i):
            return (2 * (t % 2) + i - 1) % PACK

        partners = [work.tile([P, 2, W], F32, name="partners%d" % t) for t in range(PACK)]

        def gauss(u):
            nc.scalar.activation(
                kernels[u].rearrange("p s w -> p (s w)"),
                squares[u][:].rearrange("p s w -> p (s w)"),
                ACT.Exp,
                scale=-0.5,
            )

        for t in range(PACK):
            for i, entries in enumerate((list4, list5)):
                nc.vector.tensor_scalar(
                    partners[t][:, i, :], b_windows[t][:].indirect(entries[:]), -1.0, 0.0, ALU.mult, ALU.add
                )
                difference = high[2 * (t % 2) + i]
                turn(difference, partners[t][:, i, :], b_windows[t][:, :W])
                nc.scalar.activation(squares[t // 2][:, slot(t, i), :], difference[:], ACT.Square)
            if t == 1:
                gauss(0)

        wa_mx = mx_tiles("wa")
        quantise(wa_mx, wa_grouped, 0, W)
        a_windows = windows("a")
        gt_tab_windows = windows("gt_tab")
        for t in range(PACK):
            product(low[t], (offs_words, offs_scales), wa_mx, t)
            nc.scalar.activation(a_windows[t][:, :W], low[t][:], ACT.Copy, scale=gt_column[:, t : t + 1])
        gauss(1)
        for t in reversed(range(PACK)):
            nc.scalar.activation(
                gt_tab_windows[t][:, :W], tab_windows[t][:, :W], ACT.Copy, scale=gt_column[:, t : t + 1]
            )

        weighted = [large_tile("weighted%d" % u, [P, 2, 2, W]) for u in range(2)]

        for t in range(PACK):
            turn(low[t], kernels[t // 2][:, slot(t, 0), :], kernels[t // 2][:, slot(t, 1), :])
        for t in range(PACK):
            for i in range(2):
                turned = high[2 * (t % 2) + i]
                turn(turned, partners[t][:, i, :])
                nc.vector.tensor_tensor(
                    weighted[t // 2][:, t % 2, i, :], turned[:], kernels[t // 2][:, slot(t, i), :], ALU.mult
                )
        log_denominator = squares[1]
        for t in range(PACK):
            nc.scalar.activation(log_denominator[:, t, :], low[t][:], ACT.Ln, bias=0.5)
        reciprocal = squares[0]
        nc.scalar.activation(
            reciprocal[:].rearrange("p t w -> p (t w)"),
            log_denominator[:].rearrange("p t w -> p (t w)"),
            ACT.Exp,
            scale=-1.0,
        )
        minus_gi = held.tile([P, PACK], F32, name="minus_gi")
        nc.scalar.activation(minus_gi[:], gi_column[:], ACT.Copy, scale=-1.0)
        factor = log_denominator
        for t in range(PACK):
            nc.scalar.activation(factor[:, t, :], reciprocal[:, t, :], ACT.Copy, scale=minus_gi[:, t : t + 1])

        z = z_and_kernels[:, :PACK, :]
        a_tab = work.tile([P, PACK, W], F32, name="a_tab")
        tab1 = [tab1_first] + [b_windows[t][:, :W] for t in range(1, PACK)]
        for t in range(1, PACK):
            nc.vector.tensor_copy(tab1[t], tab_windows[t][:].indirect(list1[:]))
        for t in range(PACK):
            nc.vector.tensor_tensor(a_tab[:, t, :], a_windows[t][:].indirect(list3[:]), tab1[t], ALU.mult)
            for part in halves if t == PACK - 1 else whole:
                entries = list2[:, part.start // 16 : part.stop // 16]
                nc.vector.tensor_tensor(
                    z[:, t, part], gt_tab_windows[t][:].indirect(entries), a_tab[:, t, part], ALU.add
                )
        z_grouped = reciprocal[:].rearrange("p t w -> p (t w)").bitcast(BF16)[:, : PACK * W]
        for h, part in enumerate(halves):
            nc.scalar.copy(
                z_grouped.rearrange("p (a h m t) -> p h m t a", a=PACK, h=2, t=PACK)[:, h],
                z[:, :, part].rearrange("p t (m a) -> p m t a", a=PACK),
            )

        for t in range(PACK):
            for c in range(PACK):
                for i in range(2):
                    nc.tensor.matmul(
                        low[c][:, t * P : (t + 1) * P],
                        weighted[t // 2][:, t % 2, i, c * P : (c + 1) * P],
                        identity[:],
                        start=(i == 0),
                        stop=(i == 1),
                        is_transpose=True,
                    )
        z2_grouped = grouped_tile("z2_grouped")
        for c in range(PACK):
            nc.vector.tensor_tensor(
                z2_grouped[:, c * W : (c + 1) * W].rearrange("p (c i t) -> p c t i", i=4, t=PACK),
                low[c][:].rearrange("p (t c i) -> p c t i", i=4, t=PACK),
                factor[:, :, c * P : (c + 1) * P].rearrange("p t (c i) -> p c t i", i=4),
                ALU.mult,
            )
        z_mx = mx_tiles("z")
        z2_mx = mx_tiles("z2")
        quantise(z2_mx, z2_grouped, 0, HALF)
        quantise(z_mx, z_grouped, 0, P)
        quantise(z2_mx, z2_grouped, HALF, HALF)
        quantise(z_mx, z_grouped, P, P)
        quantise(z_mx, z_grouped, HALF, HALF)

        ex_windows = windows("tab_or_ex", PACK)
        cv_windows = a_windows
        ex6 = [b_windows[t][:, :W] for t in range(PACK)]
        ex7 = factor
        pieces = [list(zip((high[0], low[0]), halves))] + [[(high[t], whole[0])] for t in range(1, PACK)]
        for t in range(PACK):
            for bank, part in pieces[t]:
                product(bank, z_mx, z2_mx, t, part)
                nc.scalar.activation(ex_windows[t][:, part], bank[:, part], ACT.Exp, scale=CV_SCALE)
        last = PACK - 1
        for t in range(SCALAR_FROM, PACK):
            nc.scalar.activation(cv_windows[t][:, :W], high[t][:], ACT.Copy, scale=CV_SCALE)
        for t in range(SCALAR_FROM, PACK):
            nc.scalar.activation(ex6[t], cv_windows[t][:].indirect(list6[:]), ACT.Exp)
        nc.scalar.activation(ex7[:, last, :], cv_windows[last][:].indirect(list7[:]), ACT.Exp)

        lower = [partners[t][:, 0, :] for t in range(PACK)]
        for t in range(last):
            nc.vector.tensor_copy(ex7[:, t, :], ex_windows[t][:].indirect(list7[:]))
            if t < SCALAR_FROM:
                nc.vector.tensor_copy(ex6[t], ex_windows[t][:].indirect(list6[:]))
        for t in range(PACK):
            nc.vector.tensor_tensor(lower[t], ex_windows[t][:].indirect(list8[:]), ex7[:, t, :], ALU.add)
        upper = low[1:] + low[:1]
        logs = [kernels[t // 2][:, 2 * (t % 2) : 2 * (t % 2) + 2, :] for t in range(PACK)]
        result = a_tab
        for t in range(PACK):
            turn(upper[t], ex6[t], ex_windows[t][:, :W])
        for t in range(PACK):
            nc.scalar.activation(logs[t][:, 0, :], upper[t][:], ACT.Ln)
            turn(high[t], logs[t][:, 0, :])
            for part in halves if t == PACK - 1 else whole:
                nc.scalar.activation(logs[t][:, 1, part], lower[t][:, part], ACT.Ln)
                nc.vector.tensor_tensor(result[:, t, part], high[t][:, part], logs[t][:, 1, part], ALU.subtract)
                nc.sync.dma_start(out_rows[:, t, part], result[:, t, part])
